import numpy as np
import ml_dtypes


def mxq(x, axis, fmt="e4m3"):
    dtype, down = {"e4m3": (ml_dtypes.float8_e4m3fn, 7), "e5m2": (ml_dtypes.float8_e5m2, 14)}[fmt]
    v = np.moveaxis(np.asarray(x, np.float32).astype(ml_dtypes.bfloat16).astype(np.float64), axis, -1)
    blocks = v.reshape(v.shape[:-1] + (-1, 32))
    amax = np.abs(blocks).max(-1, keepdims=True)
    byte = np.maximum(np.where(amax > 0, np.frexp(amax)[1] - 1 + 127, 0) - down, 1)
    scale = np.exp2(byte - 127.0)
    codes = (blocks / scale).astype(np.float32).astype(dtype).astype(np.float64)
    return np.moveaxis((codes * scale).reshape(v.shape), -1, axis)


WIDE = False


def mx_kscale(k, group=512):
    if not WIDE:
        return np.ones(k)
    levels = np.array([10, -10, 5, -5, 0])
    if group != 512:
        return np.exp2(np.random.permutation(np.resize(levels, k // group))).repeat(group)
    if k % 512:
        return np.exp2(np.random.permutation(np.resize(levels, k // 32))).repeat(32)
    a = np.empty((k // 512, 16))
    for p in range(k // 512):
        a[p, :8] = np.random.permutation(np.resize(levels, 8))
        for g in range(8):
            far = levels[np.abs(levels - a[p, g]) >= 10]
            a[p, g + 8] = far[np.random.randint(len(far))]
    return np.exp2(a.ravel()).repeat(32)


def f64(x):
    return np.asarray(x).astype(np.float64)


H, D, N = 4, 256, 512


def setup_inputs():
    n = np.random.standard_normal
    s = mx_kscale(D, 0)
    u = mx_kscale(N)
    t = np.random.uniform(0.5, 2.0, N) * u
    v = n((H, N, 128))
    v[:, :, 127] = 1.0
    return {
        "q": n((H, D, N)).astype(np.float32),
        "qa": (np.random.uniform(0.5, 2.0, D) * s)[:, None].astype(np.float32),
        "ka": np.tile(np.random.uniform(0.5, 2.0, D) / s, (128, 1)).astype(np.float32),
        "k": n((H, N, D)).astype(np.float32),
        "t": t.reshape(N, 1).astype(np.float32),
        "v": (v / t[:, None]).astype(np.float32),
        "og": n((H, N, 128)).astype(np.float32),
    }


def reference(q, qa, ka, k, t, v, og):
    fq = (np.maximum(f64(q), 0.0) + 0.125) * f64(qa)
    fk = (np.maximum(f64(k), 0.0) + 0.125) * f64(t) * f64(ka)[:1]
    S = (mxq(fk, 1, "e4m3").transpose(0, 2, 1) @ mxq(f64(v), 1, "e4m3")) / N
    y = mxq(fq, 1, "e4m3").transpose(0, 2, 1) @ mxq(S, 1, "e4m3")
    y = y / y[:, :, 127:128]
    y = y / (1.0 + np.exp(-f64(og)))
    return y

@@ -1,0 +1,222 @@
+from contextlib import ExitStack
+
+import concourse.mybir as mybir
+
+H, D, N, E = 4, 256, 512, 128
+FLOPS = 2 * 2 * H * D * N * E
+
+F32 = mybir.dt.float32
+BF16 = mybir.dt.bfloat16
+U32 = mybir.dt.uint32
+I32 = mybir.dt.int32
+U8 = mybir.dt.uint8
+FP8X4 = mybir.dt.float8_e4m3fn_x4
+ACT = mybir.ActivationFunctionType
+ALU = mybir.AluOpType
+
+P = 128
+R = 64
+PACK = 4
+PHI = 0.125
+
+ORDER = [["init"],["lt"],["la"],["lk",0,"a"],["lk",0,"b"],["T","a"],["lk",1,"w"],["K1",0,"a"],["T","b"],["K1",0,"b"],["K2",0,"a"],["lq",0],["lv",0],["lqa"],["K1",1,"w"],["Q1",0],["K2",0,"b"],["V",0,"act"],["lq",1],["zk",0],["Q1",1],["K2",1,"w"],["V",1,"dve"],["zk",1],["lk",2,"w"],["Q2",0],["zv",0],["zq",0],["K1",2,"w"],["lk",3,"w"],["lv",1],["mS",0],["Q2",1],["K1",3,"w"],["lq",2],["lq",3],["S",0],["lo",0],["V",2,"act"],["lo",1],["K2",2,"w"],["lo",2],["Q1",2],["V",3,"dve"],["K2",3,"w"],["Q1",3],["zq",1],["zk",2],["lo",3],["G",0],["zs",0],["mY",0],["zv",1],["zk",3],["Q2",2],["mS",1],["S",1],["mY",1],["Q2",3],["G",1],["rc",1],["rc",0],["zq",2],["zs",1],["Y",0,0],["zq",3],["Y",0,1],["G",2],["Y",1,1],["mY",2],["G",3],["rc",3],["mY",3],["rc",2],["Y",1,0],["st",0],["rc",5],["Y",2,1],["rc",4],["Y",2,0],["st",1],["Y",3,0],["Y",3,1],["st",2],["st",3]]
+
+
+def tile_rows_lin_relu1_norm_gate_kernel(tc, q, qa, ka, k, t, v, og, out):
+    nc = tc.nc
+    with ExitStack() as ctx:
+        sb = ctx.enter_context(tc.tile_pool(name="sb", bufs=1))
+        ps = ctx.enter_context(tc.psum_pool(name="ps", bufs=1))
+        ctx.enter_context(tc.manual_schedule())
+
+        def tiles(name, keys, shape, dtype):
+            return {key: sb.tile(shape, dtype, name="%s_%s" % (name, key), align_bytes=64) for key in keys}
+
+        heads = range(H)
+        pairs = range(2)
+        chunks = range(4)
+
+        t_sb = sb.tile([P, PACK], F32, align_bytes=64)
+        qa_sb = sb.tile([P, PACK], F32, align_bytes=64)
+        ka_sb = sb.tile([P, D], F32, align_bytes=64)
+        tka = sb.tile([P, PACK, R, PACK], F32, align_bytes=64)
+        warm = sb.tile([P, 8], F32, align_bytes=64)
+        warm2 = sb.tile([P, 8], F32, align_bytes=64)
+        k_raw = tiles("k_raw", heads, [P, PACK, D], F32)
+        k_relu = tiles("k_relu", heads, [P, PACK, R, PACK], F32)
+        k_bf = tiles("k_bf", heads, [P, PACK, R, PACK], BF16)
+        k_codes = tiles("k_codes", pairs, [P, PACK, 3 * R], U32)
+        k_scales = tiles("k_scales", pairs, [P, PACK, 3 * R], U8)
+        v_raw = tiles("v_raw", pairs, [P, 2, PACK, E], F32)
+        v_bf = tiles("v_bf", pairs, [P, 2, E, PACK], BF16)
+        v_codes = tiles("v_codes", pairs, [P, 2 * E], U32)
+        v_scales = tiles("v_scales", pairs, [P, 2 * E], U8)
+        s_bf = tiles("s_bf", pairs, [P, E, PACK], BF16)
+        s_codes = tiles("s_codes", pairs, [P, E], U32)
+        s_scales = tiles("s_scales", pairs, [P, E], U8)
+        q_raw = tiles("q_raw", chunks, [P, PACK, 2 * P], F32)
+        q_relu = tiles("q_relu", chunks, [P, 2 * P, PACK], F32)
+        q_bf = tiles("q_bf", chunks, [P, 2 * P, PACK], BF16)
+        q_codes = tiles("q_codes", chunks, [P, 2 * P], U32)
+        q_scales = tiles("q_scales", chunks, [P, 2 * P], U8)
+        og_raw = tiles("og_raw", chunks, [P, 2, 2, E], F32)
+        gate = tiles("gate", chunks, [P, 2, 2, E], F32)
+        res = tiles("res", chunks, [P, 2, 2, E], F32)
+        rden = tiles("rden", range(6), [P, 4], F32)
+        s_ps = {g: ps.tile([P, PACK, E], F32, name="s_ps_%d" % g) for g in pairs}
+        y_ps = {b: ps.tile([P, 4, E], F32, name="y_ps_%d" % b) for b in range(6)}
+
+        def y_place(ch, c):
+            if ch < 2:
+                return c, 2 * ch
+            return 2 * (ch - 1) + c, 0
+
+        def m_range(part):
+            return {"a": (0, R // 2), "b": (R // 2, R), "w": (0, R)}[part]
+
+        def init():
+            nc.gpsimd.memset(warm[:], 0.0)
+            nc.scalar.activation(out=warm2[:], in_=warm[:], func=ACT.Sigmoid)
+            for g in pairs:
+                nc.gpsimd.memset(k_codes[g][:, :, R:2 * R], 0)
+                nc.gpsimd.memset(k_scales[g][:].bitcast(I32)[:, :, R // 4:R // 2], 0)
+
+        def load_t():
+            nc.sync.dma_start(out=t_sb[:], in_=t.rearrange("(p j) o -> p (j o)", j=PACK))
+
+        def load_ka():
+            nc.sync.dma_start(out=ka_sb[:], in_=ka)
+
+        def load_qa():
+            for c in range(2):
+                nc.sync.dma_start(out=qa_sb[R * c:R * c + R, :], in_=qa.rearrange("(p j) o -> p (j o)", j=PACK))
+
+        def load_k(h, part):
+            m0, m1 = m_range(part)
+            src = k[h].rearrange("(p j) d -> p j d", j=PACK)
+            nc.sync.dma_start(out=k_raw[h][:, :, 4 * m0:4 * m1], in_=src[:, :, 4 * m0:4 * m1])
+
+        def load_v(g):
+            nc.sync.dma_start(out=v_raw[g][:].rearrange("p c j e -> p c (j e)"),
+                              in_=v[2 * g:2 * g + 2].rearrange("c (p j) e -> p c (j e)", j=PACK))
+
+        def load_q(ch):
+            g, u = divmod(ch, 2)
+            src = q[2 * g:2 * g + 2].rearrange("c (p j) n -> (c p) j n", j=PACK)
+            nc.sync.dma_start(out=q_raw[ch][:], in_=src[:, :, 2 * P * u:2 * P * (u + 1)])
+
+        def rows(x, ch):
+            g, u = divmod(ch, 2)
+            return x[2 * g:2 * g + 2, 2 * P * u:2 * P * (u + 1), :].rearrange("c (s r) e -> s c (r e)", r=2)
+
+        def load_og(ch):
+            nc.sync.dma_start(out=og_raw[ch][:].rearrange("p c r e -> p c (r e)"), in_=rows(og, ch))
+
+        def store(ch):
+            nc.sync.dma_start(out=rows(out, ch), in_=res[ch][:].rearrange("p c r e -> p c (r e)"))
+
+        def make_tka(part):
+            m0, m1 = m_range(part)
+            shape = [P, PACK, m1 - m0, PACK]
+            nc.vector.tensor_tensor(
+                out=tka[:, :, m0:m1, :],
+                in0=ka_sb[:, 4 * m0:4 * m1].rearrange("p (m x) -> p x m", x=PACK).unsqueeze(3).to_broadcast(shape),
+                in1=t_sb[:].unsqueeze(1).unsqueeze(1).to_broadcast(shape),
+                op=ALU.mult)
+
+        def relu_k(h, part):
+            m0, m1 = m_range(part)
+            nc.scalar.activation(
+                out=k_relu[h][:, :, m0:m1, :].rearrange("p x m j -> p m j x"),
+                in_=k_raw[h][:, :, 4 * m0:4 * m1].rearrange("p j (m x) -> p m j x", x=PACK),
+                func=ACT.Relu)
+
+        def scale_k(h, part):
+            m0, m1 = m_range(part)
+            nc.vector.scalar_tensor_tensor(
+                out=k_bf[h][:, :, m0:m1, :], in0=k_relu[h][:, :, m0:m1, :], scalar=PHI,
+                in1=tka[:, :, m0:m1, :], op0=ALU.add, op1=ALU.mult)
+
+        def quant_k(h):
+            g, c = divmod(h, 2)
+            cols = slice(2 * R * c, 2 * R * c + R)
+            for x in range(PACK):
+                nc.vector.quantize_mx(out=k_codes[g][:, x, cols].bitcast(FP8X4), scales=k_scales[g][:, x, cols],
+                                      in_=k_bf[h][:, x].rearrange("p m j -> p (m j)"))
+
+        def cast_v(h, eng):
+            g, c = divmod(h, 2)
+            dst = v_bf[g][:, c].rearrange("p (b i) j -> p b j i", i=4)
+            src = v_raw[g][:, c].rearrange("p j (b i) -> p b j i", i=4)
+            if eng == "act":
+                nc.scalar.copy(out=dst, in_=src)
+            else:
+                nc.vector.tensor_copy(out=dst, in_=src)
+
+        def quant_v(g):
+            nc.vector.quantize_mx(out=v_codes[g][:].bitcast(FP8X4), scales=v_scales[g][:],
+                                  in_=v_bf[g][:].rearrange("p c e j -> p (c e j)"))
+
+        def mm_state(g):
+            for x in range(PACK):
+                for c in range(2):
+                    cols = slice(R * c, R * c + P)
+                    vc = slice(E * c, E * c + E)
+                    nc.tensor.matmul_mx(out=s_ps[g][:, x, :], lhsT=k_codes[g][:, x, cols].bitcast(FP8X4),
+                                        lhsT_scale=k_scales[g][:, x, cols], rhs=v_codes[g][:, vc].bitcast(FP8X4),
+                                        rhs_scale=v_scales[g][:, vc], start=(c == 0), stop=(c == 1))
+
+        def evac_state(g):
+            nc.scalar.activation(out=s_bf[g][:], in_=s_ps[g][:].rearrange("p x e -> p e x"), func=ACT.Copy,
+                                 scale=1.0 / N)
+
+        def quant_s(g):
+            nc.vector.quantize_mx(out=s_codes[g][:].bitcast(FP8X4), scales=s_scales[g][:],
+                                  in_=s_bf[g][:].rearrange("p e x -> p (e x)"))
+
+        def relu_q(ch):
+            nc.scalar.activation(
+                out=q_relu[ch][:].rearrange("p (r s) j -> p s j r", r=2),
+                in_=q_raw[ch][:].rearrange("p j (s r) -> p s j r", r=2),
+                func=ACT.Relu)
+
+        def scale_q(ch):
+            nc.vector.scalar_tensor_tensor(
+                out=q_bf[ch][:], in0=q_relu[ch][:], scalar=PHI,
+                in1=qa_sb[:].unsqueeze(1).to_broadcast([P, 2 * P, PACK]), op0=ALU.add, op1=ALU.mult)
+
+        def quant_q(ch):
+            nc.vector.quantize_mx(out=q_codes[ch][:].bitcast(FP8X4), scales=q_scales[ch][:],
+                                  in_=q_bf[ch][:].rearrange("p n j -> p (n j)"))
+
+        def mm_read(ch):
+            g = ch // 2
+            for r in range(2):
+                for c in range(2):
+                    b, slot = y_place(ch, c)
+                    part = slice(R * c, R * c + R)
+                    cols = slice(P * r, P * r + P)
+                    nc.tensor.matmul_mx(out=y_ps[b][:, slot + r, :], lhsT=q_codes[ch][part, cols].bitcast(FP8X4),
+                                        lhsT_scale=q_scales[ch][part, cols], rhs=s_codes[g][part, :].bitcast(FP8X4),
+                                        rhs_scale=s_scales[g][part, :], start=True, stop=True)
+
+        def sigmoid(ch):
+            nc.scalar.activation(out=gate[ch][:], in_=og_raw[ch][:], func=ACT.Sigmoid)
+
+        def recip(b):
+            n = 4 if b < 2 else 2
+            nc.vector.reciprocal(out=rden[b][:, 0:n], in_=y_ps[b][:, 0:n, E - 1])
+
+        def finish(ch, c):
+            b, slot = y_place(ch, c)
+            for r in range(2):
+                nc.vector.scalar_tensor_tensor(
+                    out=res[ch][:, c, r, :], in0=y_ps[b][:, slot + r, :], scalar=rden[b][:, slot + r:slot + r + 1],
+                    in1=gate[ch][:, c, r, :], op0=ALU.mult, op1=ALU.mult)
+
+        steps = {"init": init, "lt": load_t, "la": load_ka, "lqa": load_qa, "lk": load_k, "lv": load_v, "lq": load_q, "lo": load_og, "st": store,
+                 "T": make_tka, "K1": relu_k, "K2": scale_k, "zk": quant_k, "V": cast_v, "zv": quant_v,
+                 "mS": mm_state, "S": evac_state, "zs": quant_s, "Q1": relu_q, "Q2": scale_q, "zq": quant_q,
+                 "mY": mm_read, "G": sigmoid, "rc": recip, "Y": finish}
+        for step in ORDER:
+            steps[step[0]](*step[1:])

@@ -18,8 +18,9 @@ P = 128
 R = 64
 PACK = 4
 PHI = 0.125
+BIG = 3.0e38
 
-ORDER = [["init"],["lt"],["la"],["lk",0,"a"],["lk",0,"b"],["T","a"],["lk",1,"w"],["K1",0,"a"],["T","b"],["K1",0,"b"],["K2",0,"a"],["lq",0],["lv",0],["lqa"],["K1",1,"w"],["Q1",0],["K2",0,"b"],["V",0,"act"],["lq",1],["zk",0],["Q1",1],["K2",1,"w"],["V",1,"dve"],["zk",1],["lk",2,"w"],["Q2",0],["zv",0],["zq",0],["K1",2,"w"],["lk",3,"w"],["lv",1],["mS",0],["Q2",1],["K1",3,"w"],["lq",2],["lq",3],["S",0],["lo",0],["V",2,"act"],["lo",1],["K2",2,"w"],["lo",2],["Q1",2],["V",3,"dve"],["K2",3,"w"],["Q1",3],["zq",1],["zk",2],["lo",3],["G",0],["zs",0],["mY",0],["zv",1],["zk",3],["Q2",2],["mS",1],["S",1],["mY",1],["Q2",3],["G",1],["rc",1],["rc",0],["zq",2],["zs",1],["Y",0,0],["zq",3],["Y",0,1],["G",2],["Y",1,1],["mY",2],["G",3],["rc",3],["mY",3],["rc",2],["Y",1,0],["st",0],["rc",5],["Y",2,1],["rc",4],["Y",2,0],["st",1],["Y",3,0],["Y",3,1],["st",2],["st",3]]
+ORDER = [["lt"],["lqa"],["init"],["lk",0,"a"],["la"],["lk",0,"b"],["lk",1,"w"],["lk",2,"w"],["lk",3,"w"],["lv",0],["lq",0,"w"],["lq",1,"w"],["lv",1],["lq",2,"w"],["lq",3,"w"],["lo",0],["lo",1],["lo",2],["lo",3],["qc"],["K1",0,"a"],["T","a"],["T","b"],["K1",0,"b"],["K1",1,"a"],["K2",0,"a"],["K1",1,"b"],["K2",0,"b"],["K2",1,"a"],["K1",2,"a"],["zk",0],["K1",2,"b"],["K2",1,"b"],["K1",3,"a"],["K2",2,"a"],["K1",3,"b"],["K2",2,"b"],["V",1,"act"],["K2",3,"a"],["Q1",0,"a"],["V",0,"dve"],["zk",1],["Q1",0,"b"],["zv",0],["Q1",1,"a"],["K2",3,"b"],["C",0,"a"],["zk",2],["Q1",1,"b"],["V",3,"act"],["mS",0],["C",0,"b"],["S",0],["zk",3],["C",1,"a"],["Q1",2,"a"],["V",2,"dve"],["Q2",0],["C",1,"b"],["Q1",2,"b"],["zv",1],["mS",1],["Q1",3,"a"],["Q2",1],["zs",0],["C",2,"a"],["zq",0],["Q1",3,"b"],["C",2,"b"],["zq",1],["Q2",2],["mY",0],["C",3,"a"],["S",1],["C",3,"b"],["zq",2],["mY",1],["Q2",3],["rc",0],["rc",1],["G",0],["zs",1],["G",1],["zq",3],["mY",2],["G",2],["Y",0,0],["Y",0,1],["Y",1,0],["G",3],["rc",2],["Y",1,1],["rc",3],["st",0],["Y",2,0],["mY",3],["rc",4],["st",1],["Y",2,1],["rc",5],["Y",3,0],["st",2],["Y",3,1],["st",3]]
 
 
 def tile_rows_lin_relu1_norm_gate_kernel(tc, q, qa, ka, k, t, v, og, out):
@@ -55,7 +56,12 @@ def tile_rows_lin_relu1_norm_gate_kernel(tc, q, qa, ka, k, t, v, og, out):
         s_codes = tiles("s_codes", pairs, [P, E], U32)
         s_scales = tiles("s_scales", pairs, [P, E], U8)
         q_raw = tiles("q_raw", chunks, [P, PACK, 2 * P], F32)
-        q_relu = tiles("q_relu", chunks, [P, 2 * P, PACK], F32)
+        q_aff = tiles("q_aff", chunks, [P, PACK, 2 * P], BF16)
+        q_phi = tiles("q_phi", chunks, [P, PACK, 2 * P], BF16)
+        qa8 = sb.tile([P, PACK], F32, align_bytes=64)
+        qa_side = sb.tile([P, PACK], F32, align_bytes=64)
+        q_lo = sb.tile([P, PACK], F32, align_bytes=64)
+        q_hi = sb.tile([P, PACK], F32, align_bytes=64)
         q_bf = tiles("q_bf", chunks, [P, 2 * P, PACK], BF16)
         q_codes = tiles("q_codes", chunks, [P, 2 * P], U32)
         q_scales = tiles("q_scales", chunks, [P, 2 * P], U8)
@@ -75,21 +81,21 @@ def tile_rows_lin_relu1_norm_gate_kernel(tc, q, qa, ka, k, t, v, og, out):
             return {"a": (0, R // 2), "b": (R // 2, R), "w": (0, R)}[part]
 
         def init():
-            nc.gpsimd.memset(warm[:], 0.0)
+            nc.vector.memset(warm[:], 0.0)
             nc.scalar.activation(out=warm2[:], in_=warm[:], func=ACT.Sigmoid)
             for g in pairs:
                 nc.gpsimd.memset(k_codes[g][:, :, R:2 * R], 0)
                 nc.gpsimd.memset(k_scales[g][:].bitcast(I32)[:, :, R // 4:R // 2], 0)
 
         def load_t():
-            nc.sync.dma_start(out=t_sb[:], in_=t.rearrange("(p j) o -> p (j o)", j=PACK))
+            nc.scalar.dma_start(out=t_sb[:], in_=t.rearrange("(p j) o -> p (j o)", j=PACK))
 
         def load_ka():
             nc.sync.dma_start(out=ka_sb[:], in_=ka)
 
         def load_qa():
             for c in range(2):
-                nc.sync.dma_start(out=qa_sb[R * c:R * c + R, :], in_=qa.rearrange("(p j) o -> p (j o)", j=PACK))
+                nc.scalar.dma_start(out=qa_sb[R * c:R * c + R, :], in_=qa.rearrange("(p j) o -> p (j o)", j=PACK))
 
         def load_k(h, part):
             m0, m1 = m_range(part)
@@ -100,10 +106,14 @@ def tile_rows_lin_relu1_norm_gate_kernel(tc, q, qa, ka, k, t, v, og, out):
             nc.sync.dma_start(out=v_raw[g][:].rearrange("p c j e -> p c (j e)"),
                               in_=v[2 * g:2 * g + 2].rearrange("c (p j) e -> p c (j e)", j=PACK))
 
-        def load_q(ch):
+        def j_range(part):
+            return {"a": (0, 2), "b": (2, 4), "w": (0, 4)}[part]
+
+        def load_q(ch, part):
             g, u = divmod(ch, 2)
+            j0, j1 = j_range(part)
             src = q[2 * g:2 * g + 2].rearrange("c (p j) n -> (c p) j n", j=PACK)
-            nc.sync.dma_start(out=q_raw[ch][:], in_=src[:, :, 2 * P * u:2 * P * (u + 1)])
+            nc.sync.dma_start(out=q_raw[ch][:, j0:j1, :], in_=src[:, j0:j1, 2 * P * u:2 * P * (u + 1)])
 
         def rows(x, ch):
             g, u = divmod(ch, 2)
@@ -174,16 +184,30 @@ def tile_rows_lin_relu1_norm_gate_kernel(tc, q, qa, ka, k, t, v, og, out):
             nc.vector.quantize_mx(out=s_codes[g][:].bitcast(FP8X4), scales=s_scales[g][:],
                                   in_=s_bf[g][:].rearrange("p e x -> p (e x)"))
 
-        def relu_q(ch):
-            nc.scalar.activation(
-                out=q_relu[ch][:].rearrange("p (r s) j -> p s j r", r=2),
-                in_=q_raw[ch][:].rearrange("p j (s r) -> p s j r", r=2),
-                func=ACT.Relu)
+        def q_consts():
+            nc.vector.tensor_scalar(out=qa8[:], in0=qa_sb[:], scalar1=PHI, scalar2=None, op0=ALU.mult)
+            nc.vector.tensor_scalar(out=qa_side[:], in0=qa_sb[:], scalar1=0.0, scalar2=0.5, op0=ALU.is_ge,
+                                    op1=ALU.subtract)
+            nc.vector.scalar_tensor_tensor(out=q_lo[:], in0=qa_side[:], scalar=BIG, in1=qa8[:], op0=ALU.mult,
+                                           op1=ALU.min)
+            nc.vector.scalar_tensor_tensor(out=q_hi[:], in0=qa_side[:], scalar=BIG, in1=qa8[:], op0=ALU.mult,
+                                           op1=ALU.max)
 
-        def scale_q(ch):
-            nc.vector.scalar_tensor_tensor(
-                out=q_bf[ch][:], in0=q_relu[ch][:], scalar=PHI,
-                in1=qa_sb[:].unsqueeze(1).to_broadcast([P, 2 * P, PACK]), op0=ALU.add, op1=ALU.mult)
+        def affine_q(ch, part):
+            for j in range(*j_range(part)):
+                nc.scalar.activation(
+                    out=q_aff[ch][:, j, :].rearrange("p (r s) -> p r s", r=2),
+                    in_=q_raw[ch][:, j, :].rearrange("p (s r) -> p r s", r=2),
+                    func=ACT.Identity, scale=qa_sb[:, j:j + 1], bias=qa8[:, j:j + 1])
+
+        def clamp_q(ch, part):
+            for j in range(*j_range(part)):
+                nc.vector.tensor_scalar(out=q_phi[ch][:, j, :], in0=q_aff[ch][:, j, :], scalar1=q_lo[:, j:j + 1],
+                                        scalar2=q_hi[:, j:j + 1], op0=ALU.max, op1=ALU.min)
+
+        def weave_q(ch):
+            nc.vector.tensor_copy(out=q_bf[ch][:].rearrange("p (b i) j -> p b j i", i=4),
+                                  in_=q_phi[ch][:].rearrange("p j (b i) -> p b j i", i=4))
 
         def quant_q(ch):
             nc.vector.quantize_mx(out=q_codes[ch][:].bitcast(FP8X4), scales=q_scales[ch][:],
@@ -216,7 +240,7 @@ def tile_rows_lin_relu1_norm_gate_kernel(tc, q, qa, ka, k, t, v, og, out):
 
         steps = {"init": init, "lt": load_t, "la": load_ka, "lqa": load_qa, "lk": load_k, "lv": load_v, "lq": load_q, "lo": load_og, "st": store,
                  "T": make_tka, "K1": relu_k, "K2": scale_k, "zk": quant_k, "V": cast_v, "zv": quant_v,
-                 "mS": mm_state, "S": evac_state, "zs": quant_s, "Q1": relu_q, "Q2": scale_q, "zq": quant_q,
+                 "mS": mm_state, "S": evac_state, "zs": quant_s, "Q1": affine_q, "C": clamp_q, "Q2": weave_q, "qc": q_consts, "zq": quant_q,
                  "mY": mm_read, "G": sigmoid, "rc": recip, "Y": finish}
         for step in ORDER:
             steps[step[0]](*step[1:])

@@ -20,7 +20,7 @@ PACK = 4
 PHI = 0.125
 BIG = 3.0e38
 
-ORDER = [["lt"],["lqa"],["init"],["lk",0,"a"],["la"],["lk",0,"b"],["lk",1,"w"],["lk",2,"w"],["lk",3,"w"],["lv",0],["lq",0,"w"],["lq",1,"w"],["lv",1],["lq",2,"w"],["lq",3,"w"],["lo",0],["lo",1],["lo",2],["lo",3],["qc"],["K1",0,"a"],["T","a"],["T","b"],["K1",0,"b"],["K1",1,"a"],["K2",0,"a"],["K1",1,"b"],["K2",0,"b"],["K2",1,"a"],["K1",2,"a"],["zk",0],["K1",2,"b"],["K2",1,"b"],["K1",3,"a"],["K2",2,"a"],["K1",3,"b"],["K2",2,"b"],["V",1,"act"],["K2",3,"a"],["Q1",0,"a"],["V",0,"dve"],["zk",1],["Q1",0,"b"],["zv",0],["Q1",1,"a"],["K2",3,"b"],["C",0,"a"],["zk",2],["Q1",1,"b"],["V",3,"act"],["mS",0],["C",0,"b"],["S",0],["zk",3],["C",1,"a"],["Q1",2,"a"],["V",2,"dve"],["Q2",0],["C",1,"b"],["Q1",2,"b"],["zv",1],["mS",1],["Q1",3,"a"],["Q2",1],["zs",0],["C",2,"a"],["zq",0],["Q1",3,"b"],["C",2,"b"],["zq",1],["Q2",2],["mY",0],["C",3,"a"],["S",1],["C",3,"b"],["zq",2],["mY",1],["Q2",3],["rc",0],["rc",1],["G",0],["zs",1],["G",1],["zq",3],["mY",2],["G",2],["Y",0,0],["Y",0,1],["Y",1,0],["G",3],["rc",2],["Y",1,1],["rc",3],["st",0],["Y",2,0],["mY",3],["rc",4],["st",1],["Y",2,1],["rc",5],["Y",3,0],["st",2],["Y",3,1],["st",3]]
+ORDER = [["lt"],["lqa"],["init"],["la"],["lk",0,"w"],["lk",1,"w"],["lk",2,"w"],["lk",3,"w"],["lv",0],["lq",0,"w"],["lq",1,"w"],["lv",1],["lq",2,"w"],["lq",3,"w"],["lo",0],["lo",1],["lo",2],["lo",3],["T","a"],["T","b"],["qc"],["K1",0,"a"],["K1",0,"b"],["K1",1,"a"],["K1",1,"b"],["K1",2,"a"],["K2",0,"a"],["K2",0,"b"],["K2",1,"a"],["K1",2,"b"],["K1",3,"w"],["zk",0],["K2",1,"b"],["K2",2,"a"],["V",1,"act"],["K2",2,"b"],["V",0,"dve"],["zk",1],["K2",3,"w"],["Q1",0,"a"],["zv",0],["Q1",0,"b"],["C",0,"a"],["Q1",1,"a"],["mS",0],["Q1",1,"b"],["zk",2],["V",3,"act"],["C",0,"b"],["zk",3],["C",1,"a"],["V",2,"dve"],["S",0],["Q2",0],["zv",1],["Q1",2,"a"],["C",1,"b"],["Q1",2,"b"],["Q1",3,"a"],["mS",1],["zq",0],["zs",0],["Q1",3,"b"],["Q2",1],["C",2,"a"],["S",1],["C",2,"b"],["zq",1],["Q2",2],["G",0],["mY",0],["C",3,"a"],["C",3,"b"],["zq",2],["mY",1],["G",1],["rc",0],["zs",1],["mY",2],["rc",1],["Q2",3],["Y",0,0],["Y",0,1],["st",0],["G",2],["G",3],["zq",3],["mY",3],["Y",1,0],["Y",1,1],["st",1],["rc",2],["rc",3],["Y",2,0],["su",2,0],["rc",4],["Y",2,1],["su",2,1],["rc",5],["Y",3,0],["su",3,0],["Y",3,1],["su",3,1]]
 
 
 def tile_rows_lin_relu1_norm_gate_kernel(tc, q, qa, ka, k, t, v, og, out):
@@ -124,6 +124,9 @@ def tile_rows_lin_relu1_norm_gate_kernel(tc, q, qa, ka, k, t, v, og, out):
 
         def store(ch):
             nc.sync.dma_start(out=rows(out, ch), in_=res[ch][:].rearrange("p c r e -> p c (r e)"))
+
+        def store_unit(ch, c):
+            nc.sync.dma_start(out=rows(out, ch)[:, c, :], in_=res[ch][:, c].rearrange("p r e -> p (r e)"))
 
         def make_tka(part):
             m0, m1 = m_range(part)
@@ -239,7 +242,7 @@ def tile_rows_lin_relu1_norm_gate_kernel(tc, q, qa, ka, k, t, v, og, out):
                     in1=gate[ch][:, c, r, :], op0=ALU.mult, op1=ALU.mult)
 
         steps = {"init": init, "lt": load_t, "la": load_ka, "lqa": load_qa, "lk": load_k, "lv": load_v, "lq": load_q, "lo": load_og, "st": store,
-                 "T": make_tka, "K1": relu_k, "K2": scale_k, "zk": quant_k, "V": cast_v, "zv": quant_v,
+                 "T": make_tka, "K1": relu_k, "K2": scale_k, "zk": quant_k, "su": store_unit, "V": cast_v, "zv": quant_v,
                  "mS": mm_state, "S": evac_state, "zs": quant_s, "Q1": affine_q, "C": clamp_q, "Q2": weave_q, "qc": q_consts, "zq": quant_q,
                  "mY": mm_read, "G": sigmoid, "rc": recip, "Y": finish}
         for step in ORDER:

@@ -44,7 +44,7 @@ def tile_rows_lin_relu1_norm_gate_kernel(tc, q, qa, ka, k, t, v, og, out):
         warm = sb.tile([P, 8], F32, align_bytes=64)
         warm2 = sb.tile([P, 8], F32, align_bytes=64)
         k_raw = tiles("k_raw", heads, [P, PACK, D], F32)
-        k_relu = tiles("k_relu", heads, [P, PACK, R, PACK], F32)
+        k_relu = tiles("k_relu", heads, [P, PACK, 85, PACK], F32)
         k_bf = tiles("k_bf", heads, [P, PACK, R, PACK], BF16)
         k_codes = tiles("k_codes", pairs, [P, PACK, 3 * R], U32)
         k_scales = tiles("k_scales", pairs, [P, PACK, 3 * R], U8)
@@ -57,7 +57,7 @@ def tile_rows_lin_relu1_norm_gate_kernel(tc, q, qa, ka, k, t, v, og, out):
         s_scales = tiles("s_scales", pairs, [P, E], U8)
         q_raw = tiles("q_raw", chunks, [P, PACK, 2 * P], F32)
         q_aff = tiles("q_aff", chunks, [P, PACK, 2 * P], BF16)
-        q_phi = tiles("q_phi", chunks, [P, PACK, 2 * P], BF16)
+        q_phi = tiles("q_phi", chunks, [P, PACK, 680], BF16)
         qa8 = sb.tile([P, PACK], F32, align_bytes=64)
         qa_side = sb.tile([P, PACK], F32, align_bytes=64)
         q_lo = sb.tile([P, PACK], F32, align_bytes=64)
@@ -205,12 +205,12 @@ def tile_rows_lin_relu1_norm_gate_kernel(tc, q, qa, ka, k, t, v, og, out):
 
         def clamp_q(ch, part):
             for j in range(*j_range(part)):
-                nc.vector.tensor_scalar(out=q_phi[ch][:, j, :], in0=q_aff[ch][:, j, :], scalar1=q_lo[:, j:j + 1],
+                nc.vector.tensor_scalar(out=q_phi[ch][:, j, 0:2 * P], in0=q_aff[ch][:, j, :], scalar1=q_lo[:, j:j + 1],
                                         scalar2=q_hi[:, j:j + 1], op0=ALU.max, op1=ALU.min)
 
         def weave_q(ch):
             nc.vector.tensor_copy(out=q_bf[ch][:].rearrange("p (b i) j -> p b j i", i=4),
-                                  in_=q_phi[ch][:].rearrange("p j (b i) -> p b j i", i=4))
+                                  in_=q_phi[ch][:, :, 0:2 * P].rearrange("p j (b i) -> p b j i", i=4))
 
         def quant_q(ch):
             nc.vector.quantize_mx(out=q_codes[ch][:].bitcast(FP8X4), scales=q_scales[ch][:],

@@ -20,8 +20,6 @@ PACK = 4
 PHI = 0.125
 BIG = 3.0e38
 
-ORDER = [["lt"],["lqa"],["init"],["la"],["lk",0,"w"],["lk",1,"w"],["lk",2,"w"],["lk",3,"w"],["lv",0],["lq",0,"w"],["lq",1,"w"],["lv",1],["lq",2,"w"],["lq",3,"w"],["lo",0],["lo",1],["lo",2],["lo",3],["T","a"],["T","b"],["qc"],["K1",0,"a"],["K1",0,"b"],["K1",1,"a"],["K1",1,"b"],["K1",2,"a"],["K2",0,"a"],["K2",0,"b"],["K2",1,"a"],["K1",2,"b"],["K1",3,"w"],["zk",0],["K2",1,"b"],["K2",2,"a"],["V",1,"act"],["K2",2,"b"],["V",0,"dve"],["zk",1],["K2",3,"w"],["Q1",0,"a"],["zv",0],["Q1",0,"b"],["C",0,"a"],["Q1",1,"a"],["mS",0],["Q1",1,"b"],["zk",2],["V",3,"act"],["C",0,"b"],["zk",3],["C",1,"a"],["V",2,"dve"],["S",0],["Q2",0],["zv",1],["Q1",2,"a"],["C",1,"b"],["Q1",2,"b"],["Q1",3,"a"],["mS",1],["zq",0],["zs",0],["Q1",3,"b"],["Q2",1],["C",2,"a"],["S",1],["C",2,"b"],["zq",1],["Q2",2],["G",0],["mY",0],["C",3,"a"],["C",3,"b"],["zq",2],["mY",1],["G",1],["rc",0],["zs",1],["mY",2],["rc",1],["Q2",3],["Y",0,0],["Y",0,1],["st",0],["G",2],["G",3],["zq",3],["mY",3],["Y",1,0],["Y",1,1],["st",1],["rc",2],["rc",3],["Y",2,0],["su",2,0],["rc",4],["Y",2,1],["su",2,1],["rc",5],["Y",3,0],["su",3,0],["Y",3,1],["su",3,1]]
-
 
 def tile_rows_lin_relu1_norm_gate_kernel(tc, q, qa, ka, k, t, v, og, out):
     nc = tc.nc
@@ -35,16 +33,16 @@ def tile_rows_lin_relu1_norm_gate_kernel(tc, q, qa, ka, k, t, v, og, out):
 
         heads = range(H)
         pairs = range(2)
-        chunks = range(4)
+        halves = range(4)
 
-        t_sb = sb.tile([P, PACK], F32, align_bytes=64)
-        qa_sb = sb.tile([P, PACK], F32, align_bytes=64)
-        ka_sb = sb.tile([P, D], F32, align_bytes=64)
-        tka = sb.tile([P, PACK, R, PACK], F32, align_bytes=64)
-        warm = sb.tile([P, 8], F32, align_bytes=64)
-        warm2 = sb.tile([P, 8], F32, align_bytes=64)
+        t_sb = sb.tile([P, PACK], F32, name="t_sb", align_bytes=64)
+        qa_sb = sb.tile([P, PACK], F32, name="qa_sb", align_bytes=64)
+        ka_sb = sb.tile([P, D], F32, name="ka_sb", align_bytes=64)
+        tka = sb.tile([P, PACK, R, PACK], F32, name="tka", align_bytes=64)
+        warm = sb.tile([P, 8], F32, name="warm", align_bytes=64)
+        warm2 = sb.tile([P, 8], F32, name="warm2", align_bytes=64)
         k_raw = tiles("k_raw", heads, [P, PACK, D], F32)
-        k_relu = tiles("k_relu", heads, [P, PACK, 85, PACK], F32)
+        k_relu = tiles("k_relu", heads, [P, PACK, R, PACK], F32)
         k_bf = tiles("k_bf", heads, [P, PACK, R, PACK], BF16)
         k_codes = tiles("k_codes", pairs, [P, PACK, 3 * R], U32)
         k_scales = tiles("k_scales", pairs, [P, PACK, 3 * R], U8)
@@ -55,30 +53,28 @@ def tile_rows_lin_relu1_norm_gate_kernel(tc, q, qa, ka, k, t, v, og, out):
         s_bf = tiles("s_bf", pairs, [P, E, PACK], BF16)
         s_codes = tiles("s_codes", pairs, [P, E], U32)
         s_scales = tiles("s_scales", pairs, [P, E], U8)
-        q_raw = tiles("q_raw", chunks, [P, PACK, 2 * P], F32)
-        q_aff = tiles("q_aff", chunks, [P, PACK, 2 * P], BF16)
-        q_phi = tiles("q_phi", chunks, [P, PACK, 680], BF16)
-        qa8 = sb.tile([P, PACK], F32, align_bytes=64)
-        qa_side = sb.tile([P, PACK], F32, align_bytes=64)
-        q_lo = sb.tile([P, PACK], F32, align_bytes=64)
-        q_hi = sb.tile([P, PACK], F32, align_bytes=64)
-        q_bf = tiles("q_bf", chunks, [P, 2 * P, PACK], BF16)
-        q_codes = tiles("q_codes", chunks, [P, 2 * P], U32)
-        q_scales = tiles("q_scales", chunks, [P, 2 * P], U8)
-        og_raw = tiles("og_raw", chunks, [P, 2, 2, E], F32)
-        gate = tiles("gate", chunks, [P, 2, 2, E], F32)
-        res = tiles("res", chunks, [P, 2, 2, E], F32)
+        q_raw = tiles("q_raw", halves, [P, 2, N], F32)
+        q_aff = tiles("q_aff", pairs, [P, PACK, N], BF16)
+        q_phi = tiles("q_phi", pairs, [P, PACK, N], BF16)
+        qa8 = sb.tile([P, PACK], F32, name="qa8", align_bytes=64)
+        qa_side = sb.tile([P, PACK], F32, name="qa_side", align_bytes=64)
+        q_lo = sb.tile([P, PACK], F32, name="q_lo", align_bytes=64)
+        q_hi = sb.tile([P, PACK], F32, name="q_hi", align_bytes=64)
+        q_bf = tiles("q_bf", halves, [P, 2, P, PACK], BF16)
+        q_codes = tiles("q_codes", halves, [P, 2 * P], U32)
+        q_scales = tiles("q_scales", halves, [P, 2 * P], U8)
+        og_raw = tiles("og_raw", pairs, [P, 2, PACK, E], F32)
+        gate = tiles("gate", pairs, [P, 2, PACK, E], F32)
+        res = tiles("res", pairs, [P, 2, PACK, E], F32)
+        ynorm = tiles("ynorm", pairs, [P, 2, PACK, E], F32)
         rden = tiles("rden", range(6), [P, 4], F32)
         s_ps = {g: ps.tile([P, PACK, E], F32, name="s_ps_%d" % g) for g in pairs}
         y_ps = {b: ps.tile([P, 4, E], F32, name="y_ps_%d" % b) for b in range(6)}
 
-        def y_place(ch, c):
-            if ch < 2:
-                return c, 2 * ch
-            return 2 * (ch - 1) + c, 0
-
-        def m_range(part):
-            return {"a": (0, R // 2), "b": (R // 2, R), "w": (0, R)}[part]
+        def y_place(half, c):
+            if half < 2:
+                return c, 2 * half
+            return 2 * (half - 1) + c, 0
 
         def init():
             nc.vector.memset(warm[:], 0.0)
@@ -97,39 +93,28 @@ def tile_rows_lin_relu1_norm_gate_kernel(tc, q, qa, ka, k, t, v, og, out):
             for c in range(2):
                 nc.scalar.dma_start(out=qa_sb[R * c:R * c + R, :], in_=qa.rearrange("(p j) o -> p (j o)", j=PACK))
 
-        def load_k(h, part):
-            m0, m1 = m_range(part)
-            src = k[h].rearrange("(p j) d -> p j d", j=PACK)
-            nc.sync.dma_start(out=k_raw[h][:, :, 4 * m0:4 * m1], in_=src[:, :, 4 * m0:4 * m1])
+        def load_k(h):
+            nc.sync.dma_start(out=k_raw[h][:], in_=k[h].rearrange("(p j) d -> p j d", j=PACK))
+
+        def rows(x, g):
+            return x[2 * g:2 * g + 2].rearrange("c (p j) e -> p c (j e)", j=PACK)
 
         def load_v(g):
-            nc.sync.dma_start(out=v_raw[g][:].rearrange("p c j e -> p c (j e)"),
-                              in_=v[2 * g:2 * g + 2].rearrange("c (p j) e -> p c (j e)", j=PACK))
+            nc.sync.dma_start(out=v_raw[g][:].rearrange("p c j e -> p c (j e)"), in_=rows(v, g))
 
-        def j_range(part):
-            return {"a": (0, 2), "b": (2, 4), "w": (0, 4)}[part]
-
-        def load_q(ch, part):
-            g, u = divmod(ch, 2)
-            j0, j1 = j_range(part)
+        def load_q(half):
+            g, u = divmod(half, 2)
             src = q[2 * g:2 * g + 2].rearrange("c (p j) n -> (c p) j n", j=PACK)
-            nc.sync.dma_start(out=q_raw[ch][:, j0:j1, :], in_=src[:, j0:j1, 2 * P * u:2 * P * (u + 1)])
+            nc.sync.dma_start(out=q_raw[half][:], in_=src[:, 2 * u:2 * u + 2, :])
 
-        def rows(x, ch):
-            g, u = divmod(ch, 2)
-            return x[2 * g:2 * g + 2, 2 * P * u:2 * P * (u + 1), :].rearrange("c (s r) e -> s c (r e)", r=2)
+        def load_og(g):
+            nc.sync.dma_start(out=og_raw[g][:].rearrange("p c r e -> p c (r e)"), in_=rows(og, g))
 
-        def load_og(ch):
-            nc.sync.dma_start(out=og_raw[ch][:].rearrange("p c r e -> p c (r e)"), in_=rows(og, ch))
+        def store(g, c0, c1, r0, r1):
+            nc.sync.dma_start(out=rows(out, g)[:, c0:c1, E * r0:E * r1],
+                              in_=res[g][:].rearrange("p c r e -> p c (r e)")[:, c0:c1, E * r0:E * r1])
 
-        def store(ch):
-            nc.sync.dma_start(out=rows(out, ch), in_=res[ch][:].rearrange("p c r e -> p c (r e)"))
-
-        def store_unit(ch, c):
-            nc.sync.dma_start(out=rows(out, ch)[:, c, :], in_=res[ch][:, c].rearrange("p r e -> p (r e)"))
-
-        def make_tka(part):
-            m0, m1 = m_range(part)
+        def make_tka(m0, m1):
             shape = [P, PACK, m1 - m0, PACK]
             nc.vector.tensor_tensor(
                 out=tka[:, :, m0:m1, :],
@@ -137,15 +122,19 @@ def tile_rows_lin_relu1_norm_gate_kernel(tc, q, qa, ka, k, t, v, og, out):
                 in1=t_sb[:].unsqueeze(1).unsqueeze(1).to_broadcast(shape),
                 op=ALU.mult)
 
-        def relu_k(h, part):
-            m0, m1 = m_range(part)
-            nc.scalar.activation(
-                out=k_relu[h][:, :, m0:m1, :].rearrange("p x m j -> p m j x"),
-                in_=k_raw[h][:, :, 4 * m0:4 * m1].rearrange("p j (m x) -> p m j x", x=PACK),
-                func=ACT.Relu)
+        def relu_views(h, m0, m1):
+            return (k_relu[h][:, :, m0:m1, :].rearrange("p x m j -> p m j x"),
+                    k_raw[h][:, :, 4 * m0:4 * m1].rearrange("p j (m x) -> p m j x", x=PACK))
 
-        def scale_k(h, part):
-            m0, m1 = m_range(part)
+        def relu_k(h, m0=0, m1=R):
+            dst, src = relu_views(h, m0, m1)
+            nc.scalar.activation(out=dst, in_=src, func=ACT.Relu)
+
+        def relu_k_vector(h, m0, m1):
+            dst, src = relu_views(h, m0, m1)
+            nc.vector.tensor_scalar(out=dst, in0=src, scalar1=0.0, scalar2=None, op0=ALU.max)
+
+        def scale_k(h, m0=0, m1=R):
             nc.vector.scalar_tensor_tensor(
                 out=k_bf[h][:, :, m0:m1, :], in0=k_relu[h][:, :, m0:m1, :], scalar=PHI,
                 in1=tka[:, :, m0:m1, :], op0=ALU.add, op1=ALU.mult)
@@ -157,14 +146,18 @@ def tile_rows_lin_relu1_norm_gate_kernel(tc, q, qa, ka, k, t, v, og, out):
                 nc.vector.quantize_mx(out=k_codes[g][:, x, cols].bitcast(FP8X4), scales=k_scales[g][:, x, cols],
                                       in_=k_bf[h][:, x].rearrange("p m j -> p (m j)"))
 
-        def cast_v(h, eng):
+        def v_views(h):
             g, c = divmod(h, 2)
-            dst = v_bf[g][:, c].rearrange("p (b i) j -> p b j i", i=4)
-            src = v_raw[g][:, c].rearrange("p j (b i) -> p b j i", i=4)
-            if eng == "act":
-                nc.scalar.copy(out=dst, in_=src)
-            else:
-                nc.vector.tensor_copy(out=dst, in_=src)
+            return (v_bf[g][:, c].rearrange("p (b i) j -> p b j i", i=4),
+                    v_raw[g][:, c].rearrange("p j (b i) -> p b j i", i=4))
+
+        def cast_v(h):
+            dst, src = v_views(h)
+            nc.scalar.copy(out=dst, in_=src)
+
+        def cast_v_vector(h):
+            dst, src = v_views(h)
+            nc.vector.tensor_copy(out=dst, in_=src)
 
         def quant_v(g):
             nc.vector.quantize_mx(out=v_codes[g][:].bitcast(FP8X4), scales=v_scales[g][:],
@@ -183,67 +176,194 @@ def tile_rows_lin_relu1_norm_gate_kernel(tc, q, qa, ka, k, t, v, og, out):
             nc.scalar.activation(out=s_bf[g][:], in_=s_ps[g][:].rearrange("p x e -> p e x"), func=ACT.Copy,
                                  scale=1.0 / N)
 
+        def evac_state_vector(g):
+            nc.vector.tensor_scalar(out=s_bf[g][:], in0=s_ps[g][:].rearrange("p x e -> p e x"), scalar1=1.0 / N,
+                                    scalar2=None, op0=ALU.mult)
+
         def quant_s(g):
             nc.vector.quantize_mx(out=s_codes[g][:].bitcast(FP8X4), scales=s_scales[g][:],
                                   in_=s_bf[g][:].rearrange("p e x -> p (e x)"))
 
-        def q_consts():
+        def q_consts_a():
             nc.vector.tensor_scalar(out=qa8[:], in0=qa_sb[:], scalar1=PHI, scalar2=None, op0=ALU.mult)
             nc.vector.tensor_scalar(out=qa_side[:], in0=qa_sb[:], scalar1=0.0, scalar2=0.5, op0=ALU.is_ge,
                                     op1=ALU.subtract)
+
+        def q_consts_b():
             nc.vector.scalar_tensor_tensor(out=q_lo[:], in0=qa_side[:], scalar=BIG, in1=qa8[:], op0=ALU.mult,
                                            op1=ALU.min)
             nc.vector.scalar_tensor_tensor(out=q_hi[:], in0=qa_side[:], scalar=BIG, in1=qa8[:], op0=ALU.mult,
                                            op1=ALU.max)
 
-        def affine_q(ch, part):
-            for j in range(*j_range(part)):
-                nc.scalar.activation(
-                    out=q_aff[ch][:, j, :].rearrange("p (r s) -> p r s", r=2),
-                    in_=q_raw[ch][:, j, :].rearrange("p (s r) -> p r s", r=2),
-                    func=ACT.Identity, scale=qa_sb[:, j:j + 1], bias=qa8[:, j:j + 1])
+        def affine_q(g, j):
+            nc.scalar.activation(out=q_aff[g][:, j, :], in_=q_raw[2 * g + j // 2][:, j % 2, :],
+                                 func=ACT.Identity, scale=qa_sb[:, j:j + 1], bias=qa8[:, j:j + 1])
 
-        def clamp_q(ch, part):
-            for j in range(*j_range(part)):
-                nc.vector.tensor_scalar(out=q_phi[ch][:, j, 0:2 * P], in0=q_aff[ch][:, j, :], scalar1=q_lo[:, j:j + 1],
-                                        scalar2=q_hi[:, j:j + 1], op0=ALU.max, op1=ALU.min)
+        def affine_q_vector(g, j):
+            nc.vector.tensor_scalar(out=q_aff[g][:, j, :], in0=q_raw[2 * g + j // 2][:, j % 2, :],
+                                    scalar1=qa_sb[:, j:j + 1], scalar2=qa8[:, j:j + 1], op0=ALU.mult, op1=ALU.add)
 
-        def weave_q(ch):
-            nc.vector.tensor_copy(out=q_bf[ch][:].rearrange("p (b i) j -> p b j i", i=4),
-                                  in_=q_phi[ch][:, :, 0:2 * P].rearrange("p j (b i) -> p b j i", i=4))
+        def clamp_q(g, j):
+            nc.vector.tensor_scalar(out=q_phi[g][:, j, :], in0=q_aff[g][:, j, :], scalar1=q_lo[:, j:j + 1],
+                                    scalar2=q_hi[:, j:j + 1], op0=ALU.max, op1=ALU.min)
 
-        def quant_q(ch):
-            nc.vector.quantize_mx(out=q_codes[ch][:].bitcast(FP8X4), scales=q_scales[ch][:],
-                                  in_=q_bf[ch][:].rearrange("p n j -> p (n j)"))
+        def weave_views(half):
+            g, u = divmod(half, 2)
+            src = q_phi[g][:].rearrange("p j (b i r) -> p b j i r", i=2, r=4)[:, :, :, :, 2 * u:2 * u + 2]
+            return q_bf[half][:].rearrange("p r (b i) j -> p b j i r", i=2), src
 
-        def mm_read(ch):
-            g = ch // 2
-            for r in range(2):
-                for c in range(2):
-                    b, slot = y_place(ch, c)
+        def weave_q(half):
+            dst, src = weave_views(half)
+            nc.vector.tensor_copy(out=dst, in_=src)
+
+        def weave_q_scalar(half):
+            dst, src = weave_views(half)
+            nc.scalar.copy(out=dst, in_=src)
+
+        def weave_q_gpsimd(half):
+            dst, src = weave_views(half)
+            nc.gpsimd.tensor_scalar(out=dst, in0=src, scalar1=1.0, scalar2=0.0, op0=ALU.mult, op1=ALU.add)
+
+        def quant_q(half):
+            nc.vector.quantize_mx(out=q_codes[half][:].bitcast(FP8X4), scales=q_scales[half][:],
+                                  in_=q_bf[half][:].rearrange("p r n j -> p (r n j)"))
+
+        def mm_read(half):
+            g = half // 2
+            for c in range(2):
+                for r in range(2):
+                    b, slot = y_place(half, c)
                     part = slice(R * c, R * c + R)
                     cols = slice(P * r, P * r + P)
-                    nc.tensor.matmul_mx(out=y_ps[b][:, slot + r, :], lhsT=q_codes[ch][part, cols].bitcast(FP8X4),
-                                        lhsT_scale=q_scales[ch][part, cols], rhs=s_codes[g][part, :].bitcast(FP8X4),
+                    nc.tensor.matmul_mx(out=y_ps[b][:, slot + r, :], lhsT=q_codes[half][part, cols].bitcast(FP8X4),
+                                        lhsT_scale=q_scales[half][part, cols], rhs=s_codes[g][part, :].bitcast(FP8X4),
                                         rhs_scale=s_scales[g][part, :], start=True, stop=True)
 
-        def sigmoid(ch):
-            nc.scalar.activation(out=gate[ch][:], in_=og_raw[ch][:], func=ACT.Sigmoid)
+        def sigmoid(g, c0, c1, r0, r1):
+            nc.scalar.activation(out=gate[g][:, c0:c1, r0:r1, :], in_=og_raw[g][:, c0:c1, r0:r1, :], func=ACT.Sigmoid)
 
         def recip(b):
             n = 4 if b < 2 else 2
             nc.vector.reciprocal(out=rden[b][:, 0:n], in_=y_ps[b][:, 0:n, E - 1])
 
-        def finish(ch, c):
-            b, slot = y_place(ch, c)
+        def finish(half, c):
+            g, u = divmod(half, 2)
+            b, slot = y_place(half, c)
             for r in range(2):
                 nc.vector.scalar_tensor_tensor(
-                    out=res[ch][:, c, r, :], in0=y_ps[b][:, slot + r, :], scalar=rden[b][:, slot + r:slot + r + 1],
-                    in1=gate[ch][:, c, r, :], op0=ALU.mult, op1=ALU.mult)
+                    out=res[g][:, c, 2 * u + r, :], in0=y_ps[b][:, slot + r, :],
+                    scalar=rden[b][:, slot + r:slot + r + 1],
+                    in1=gate[g][:, c, 2 * u + r, :], op0=ALU.mult, op1=ALU.mult)
 
-        steps = {"init": init, "lt": load_t, "la": load_ka, "lqa": load_qa, "lk": load_k, "lv": load_v, "lq": load_q, "lo": load_og, "st": store,
-                 "T": make_tka, "K1": relu_k, "K2": scale_k, "zk": quant_k, "su": store_unit, "V": cast_v, "zv": quant_v,
-                 "mS": mm_state, "S": evac_state, "zs": quant_s, "Q1": affine_q, "C": clamp_q, "Q2": weave_q, "qc": q_consts, "zq": quant_q,
-                 "mY": mm_read, "G": sigmoid, "rc": recip, "Y": finish}
-        for step in ORDER:
-            steps[step[0]](*step[1:])
+        def normalise(half, c):
+            g, u = divmod(half, 2)
+            b, slot = y_place(half, c)
+            for r in range(2):
+                nc.scalar.activation(out=ynorm[g][:, c, 2 * u + r, :], in_=y_ps[b][:, slot + r, :], func=ACT.Copy,
+                                     scale=rden[b][:, slot + r:slot + r + 1])
+
+        def gate_gpsimd(half, c):
+            g, u = divmod(half, 2)
+            nc.gpsimd.tensor_tensor(out=res[g][:, c, 2 * u:2 * u + 2, :], in0=ynorm[g][:, c, 2 * u:2 * u + 2, :],
+                                    in1=gate[g][:, c, 2 * u:2 * u + 2, :], op=ALU.mult)
+
+        load_t()
+        load_qa()
+        init()
+        load_ka()
+        load_k(0)
+        load_k(1)
+        load_v(0)
+        load_k(2)
+        load_k(3)
+        load_q(0)
+        load_q(1)
+        load_v(1)
+        load_q(2)
+        load_q(3)
+        load_og(0)
+        load_og(1)
+        make_tka(0, R)
+        relu_k_vector(0, 0, 16)
+        q_consts_a()
+        relu_k(0, 16, 40)
+        relu_k(0, 40, 64)
+        scale_k(0, 0, 16)
+        scale_k(0, 16, 40)
+        scale_k(0, 40, 64)
+        q_consts_b()
+        relu_k(1, 0, 32)
+        relu_k(1, 32, 64)
+        quant_k(0)
+        scale_k(1, 0, 32)
+        scale_k(1, 32, 64)
+        cast_v(0)
+        cast_v_vector(1)
+        quant_k(1)
+        quant_v(0)
+        mm_state(0)
+        relu_k(2, 0, 32)
+        relu_k(2, 32, 64)
+        scale_k(2, 0, 32)
+        scale_k(2, 32, 64)
+        relu_k(3, 0, 32)
+        relu_k(3, 32, 64)
+        scale_k(3, 0, 32)
+        quant_k(2)
+        scale_k(3, 32, 64)
+        for j in range(3):
+            affine_q(0, j)
+        affine_q_vector(0, 3)
+        quant_k(3)
+        for j in (0, 1, 3, 2):
+            clamp_q(0, j)
+        evac_state(0)
+        cast_v(2)
+        cast_v(3)
+        quant_s(0)
+        weave_q(0)
+        weave_q(1)
+        quant_v(1)
+        mm_state(1)
+        quant_q(0)
+        mm_read(0)
+        quant_q(1)
+        mm_read(1)
+        affine_q(1, 0)
+        affine_q(1, 1)
+        affine_q(1, 2)
+        affine_q_vector(1, 3)
+        for j in (0, 1, 3, 2):
+            clamp_q(1, j)
+        sigmoid(0, 0, 1, 0, 4)
+        evac_state(1)
+        weave_q_scalar(3)
+        weave_q(2)
+        recip(0)
+        recip(1)
+        quant_s(1)
+        quant_q(2)
+        mm_read(2)
+        sigmoid(0, 1, 2, 0, 4)
+        sigmoid(1, 0, 2, 0, 2)
+        sigmoid(1, 0, 2, 2, 4)
+        finish(0, 0)
+        finish(1, 0)
+        quant_q(3)
+        mm_read(3)
+        store(0, 0, 1, 0, 4)
+        finish(0, 1)
+        recip(2)
+        recip(3)
+        finish(1, 1)
+        store(0, 1, 2, 0, 4)
+        finish(2, 0)
+        store(1, 0, 1, 0, 2)
+        recip(4)
+        recip(5)
+        finish(2, 1)
+        store(1, 1, 2, 0, 2)
+        finish(3, 0)
+        store(1, 0, 1, 2, 4)
+        finish(3, 1)
+        store(1, 1, 2, 2, 4)

@@ -53,7 +53,11 @@ def tile_rows_lin_relu1_norm_gate_kernel(tc, q, qa, ka, k, t, v, og, out):
         s_bf = tiles("s_bf", pairs, [P, E, PACK], BF16)
         s_codes = tiles("s_codes", pairs, [P, E], U32)
         s_scales = tiles("s_scales", pairs, [P, E], U8)
-        q_raw = tiles("q_raw", halves, [P, 2, N], F32)
+        BYROW = [1,1]
+        q_raw = {}
+        for half in halves:
+            q_raw[half] = sb.tile([P, 2, N] if BYROW[half // 2] else [P, PACK, N // 2], F32, name="q_raw_%d" % half,
+                                  align_bytes=64)
         q_aff = tiles("q_aff", pairs, [P, PACK, N], BF16)
         q_phi = tiles("q_phi", pairs, [P, PACK, N], BF16)
         qa8 = sb.tile([P, PACK], F32, name="qa8", align_bytes=64)
@@ -99,20 +103,30 @@ def tile_rows_lin_relu1_norm_gate_kernel(tc, q, qa, ka, k, t, v, og, out):
         def rows(x, g):
             return x[2 * g:2 * g + 2].rearrange("c (p j) e -> p c (j e)", j=PACK)
 
+        def rows2(x, g):
+            return x[2 * g:2 * g + 2].rearrange("c (u s r) e -> s (c u) (r e)", u=2, r=2)
+
         def load_v(g):
             nc.sync.dma_start(out=v_raw[g][:].rearrange("p c j e -> p c (j e)"), in_=rows(v, g))
 
         def load_q(half):
             g, u = divmod(half, 2)
             src = q[2 * g:2 * g + 2].rearrange("c (p j) n -> (c p) j n", j=PACK)
-            nc.sync.dma_start(out=q_raw[half][:], in_=src[:, 2 * u:2 * u + 2, :])
+            if BYROW[g]:
+                nc.sync.dma_start(out=q_raw[half][:], in_=src[:, 2 * u:2 * u + 2, :])
+            else:
+                nc.sync.dma_start(out=q_raw[half][:], in_=src[:, :, 2 * P * u:2 * P * (u + 1)])
 
         def load_og(g):
-            nc.sync.dma_start(out=og_raw[g][:].rearrange("p c r e -> p c (r e)"), in_=rows(og, g))
+            nc.sync.dma_start(out=og_raw[g][:].rearrange("p c (u r) e -> p (c u) (r e)", u=2), in_=rows2(og, g))
 
         def store(g, c0, c1, r0, r1):
-            nc.sync.dma_start(out=rows(out, g)[:, c0:c1, E * r0:E * r1],
-                              in_=res[g][:].rearrange("p c r e -> p c (r e)")[:, c0:c1, E * r0:E * r1])
+            dst = rows2(out, g).rearrange("s (c u) x -> s c u x", u=2)
+            src = res[g][:].rearrange("p c (u r) e -> p c u (r e)", u=2)
+            if r1 - r0 == 4:
+                nc.sync.dma_start(out=dst[:, c0], in_=src[:, c0])
+            else:
+                nc.sync.dma_start(out=dst[:, c0:c1, r0 // 2], in_=src[:, c0:c1, r0 // 2])
 
         def make_tka(m0, m1):
             shape = [P, PACK, m1 - m0, PACK]
@@ -195,33 +209,48 @@ def tile_rows_lin_relu1_norm_gate_kernel(tc, q, qa, ka, k, t, v, og, out):
             nc.vector.scalar_tensor_tensor(out=q_hi[:], in0=qa_side[:], scalar=BIG, in1=qa8[:], op0=ALU.mult,
                                            op1=ALU.max)
 
-        def affine_q(g, j):
-            nc.scalar.activation(out=q_aff[g][:, j, :], in_=q_raw[2 * g + j // 2][:, j % 2, :],
-                                 func=ACT.Identity, scale=qa_sb[:, j:j + 1], bias=qa8[:, j:j + 1])
+        def affine_views(g, j, u):
+            if BYROW[g]:
+                return (q_aff[g][:, j, :].rearrange("p (u r s) -> p u r s", u=2, r=2),
+                        q_raw[2 * g + j // 2][:, j % 2, :].rearrange("p (u s r) -> p u r s", u=2, r=2))
+            return (q_aff[g][:, j, 2 * P * u:2 * P * (u + 1)].rearrange("p (r s) -> p r s", r=2),
+                    q_raw[2 * g + u][:, j, :].rearrange("p (s r) -> p r s", r=2))
 
-        def affine_q_vector(g, j):
-            nc.vector.tensor_scalar(out=q_aff[g][:, j, :], in0=q_raw[2 * g + j // 2][:, j % 2, :],
-                                    scalar1=qa_sb[:, j:j + 1], scalar2=qa8[:, j:j + 1], op0=ALU.mult, op1=ALU.add)
+        def affine_q(g, j, u=0):
+            dst, src = affine_views(g, j, u)
+            nc.scalar.activation(out=dst, in_=src, func=ACT.Identity, scale=qa_sb[:, j:j + 1], bias=qa8[:, j:j + 1])
 
-        def clamp_q(g, j):
-            nc.vector.tensor_scalar(out=q_phi[g][:, j, :], in0=q_aff[g][:, j, :], scalar1=q_lo[:, j:j + 1],
+        def affine_q_vector(g, j, u=0):
+            dst, src = affine_views(g, j, u)
+            nc.vector.tensor_scalar(out=dst, in0=src, scalar1=qa_sb[:, j:j + 1], scalar2=qa8[:, j:j + 1],
+                                    op0=ALU.mult, op1=ALU.add)
+
+        def affine_q_gpsimd(g, j, u=0):
+            dst, src = affine_views(g, j, u)
+            nc.gpsimd.tensor_scalar(out=dst, in0=src, scalar1=qa_sb[:, j:j + 1], scalar2=qa8[:, j:j + 1],
+                                    op0=ALU.mult, op1=ALU.add)
+
+        def clamp_q(g, j, u=0):
+            cols = slice(0, N) if BYROW[g] else slice(2 * P * u, 2 * P * (u + 1))
+            nc.vector.tensor_scalar(out=q_phi[g][:, j, cols], in0=q_aff[g][:, j, cols], scalar1=q_lo[:, j:j + 1],
                                     scalar2=q_hi[:, j:j + 1], op0=ALU.max, op1=ALU.min)
 
-        def weave_views(half):
+        def weave_views(half, n0, n1):
             g, u = divmod(half, 2)
-            src = q_phi[g][:].rearrange("p j (b i r) -> p b j i r", i=2, r=4)[:, :, :, :, 2 * u:2 * u + 2]
-            return q_bf[half][:].rearrange("p r (b i) j -> p b j i r", i=2), src
+            src = q_phi[g][:, :, 2 * P * u + n0:2 * P * u + n1].rearrange("p j (b i) -> p b j i", i=4)
+            dst = q_bf[half][:].rearrange("p r s j -> p (r s) j")[:, n0:n1, :]
+            return dst.rearrange("p (b i) j -> p b j i", i=4), src
 
-        def weave_q(half):
-            dst, src = weave_views(half)
+        def weave_q(half, n0=0, n1=2 * P):
+            dst, src = weave_views(half, n0, n1)
             nc.vector.tensor_copy(out=dst, in_=src)
 
-        def weave_q_scalar(half):
-            dst, src = weave_views(half)
+        def weave_q_scalar(half, n0=0, n1=2 * P):
+            dst, src = weave_views(half, n0, n1)
             nc.scalar.copy(out=dst, in_=src)
 
-        def weave_q_gpsimd(half):
-            dst, src = weave_views(half)
+        def weave_q_gpsimd(half, n0=0, n1=2 * P):
+            dst, src = weave_views(half, n0, n1)
             nc.gpsimd.tensor_scalar(out=dst, in0=src, scalar1=1.0, scalar2=0.0, op0=ALU.mult, op1=ALU.add)
 
         def quant_q(half):
@@ -267,14 +296,18 @@ def tile_rows_lin_relu1_norm_gate_kernel(tc, q, qa, ka, k, t, v, og, out):
             nc.gpsimd.tensor_tensor(out=res[g][:, c, 2 * u:2 * u + 2, :], in0=ynorm[g][:, c, 2 * u:2 * u + 2, :],
                                     in1=gate[g][:, c, 2 * u:2 * u + 2, :], op=ALU.mult)
 
+        def finish_aside(half, c):
+            normalise(half, c)
+            gate_gpsimd(half, c)
+
         load_t()
         load_qa()
         init()
         load_ka()
         load_k(0)
         load_k(1)
-        load_v(0)
         load_k(2)
+        load_v(0)
         load_k(3)
         load_q(0)
         load_q(1)
@@ -297,19 +330,17 @@ def tile_rows_lin_relu1_norm_gate_kernel(tc, q, qa, ka, k, t, v, og, out):
         quant_k(0)
         scale_k(1, 0, 32)
         scale_k(1, 32, 64)
+        relu_k(2, 0, 64)
         cast_v(0)
         cast_v_vector(1)
         quant_k(1)
+        scale_k(2, 0, 64)
         quant_v(0)
         mm_state(0)
-        relu_k(2, 0, 32)
-        relu_k(2, 32, 64)
-        scale_k(2, 0, 32)
-        scale_k(2, 32, 64)
+        quant_k(2)
         relu_k(3, 0, 32)
         relu_k(3, 32, 64)
         scale_k(3, 0, 32)
-        quant_k(2)
         scale_k(3, 32, 64)
         for j in range(3):
             affine_q(0, j)
@@ -319,38 +350,39 @@ def tile_rows_lin_relu1_norm_gate_kernel(tc, q, qa, ka, k, t, v, og, out):
             clamp_q(0, j)
         evac_state(0)
         cast_v(2)
-        cast_v(3)
+        cast_v_vector(3)
         quant_s(0)
         weave_q(0)
-        weave_q(1)
         quant_v(1)
         mm_state(1)
+        weave_q(1)
         quant_q(0)
         mm_read(0)
-        quant_q(1)
-        mm_read(1)
         affine_q(1, 0)
         affine_q(1, 1)
         affine_q(1, 2)
         affine_q_vector(1, 3)
         for j in (0, 1, 3, 2):
             clamp_q(1, j)
-        sigmoid(0, 0, 1, 0, 4)
+        quant_q(1)
+        mm_read(1)
         evac_state(1)
-        weave_q_scalar(3)
-        weave_q(2)
-        recip(0)
-        recip(1)
-        quant_s(1)
-        quant_q(2)
-        mm_read(2)
+        sigmoid(0, 0, 1, 0, 4)
+        weave_q_scalar(3, 64, 256)
         sigmoid(0, 1, 2, 0, 4)
         sigmoid(1, 0, 2, 0, 2)
         sigmoid(1, 0, 2, 2, 4)
+        weave_q(2)
+        quant_s(1)
+        weave_q(3, 0, 64)
+        quant_q(2)
+        mm_read(2)
+        recip(0)
+        recip(1)
         finish(0, 0)
-        finish(1, 0)
         quant_q(3)
         mm_read(3)
+        finish(1, 0)
         store(0, 0, 1, 0, 4)
         finish(0, 1)
         recip(2)

@@ -332,7 +332,7 @@ def tile_rows_lin_relu1_norm_gate_kernel(tc, q, qa, ka, k, t, v, og, out):
         scale_k(1, 32, 64)
         relu_k(2, 0, 64)
         cast_v(0)
-        cast_v_vector(1)
+        cast_v(1)
         quant_k(1)
         scale_k(2, 0, 64)
         quant_v(0)
@@ -351,11 +351,12 @@ def tile_rows_lin_relu1_norm_gate_kernel(tc, q, qa, ka, k, t, v, og, out):
         evac_state(0)
         cast_v(2)
         cast_v_vector(3)
+        weave_q_scalar(1, 128, 256)
         quant_s(0)
         weave_q(0)
         quant_v(1)
         mm_state(1)
-        weave_q(1)
+        weave_q(1, 0, 128)
         quant_q(0)
         mm_read(0)
         affine_q(1, 0)
@@ -367,28 +368,29 @@ def tile_rows_lin_relu1_norm_gate_kernel(tc, q, qa, ka, k, t, v, og, out):
         quant_q(1)
         mm_read(1)
         evac_state(1)
-        sigmoid(0, 0, 1, 0, 4)
-        weave_q_scalar(3, 64, 256)
         sigmoid(0, 1, 2, 0, 4)
-        sigmoid(1, 0, 2, 0, 2)
-        sigmoid(1, 0, 2, 2, 4)
+        weave_q_scalar(3, 128, 256)
+        sigmoid(0, 0, 1, 0, 4)
         weave_q(2)
         quant_s(1)
-        weave_q(3, 0, 64)
+        weave_q(3, 0, 128)
+        recip(1)
         quant_q(2)
         mm_read(2)
         recip(0)
-        recip(1)
-        finish(0, 0)
         quant_q(3)
         mm_read(3)
-        finish(1, 0)
-        store(0, 0, 1, 0, 4)
         finish(0, 1)
+        store(0, 1, 2, 0, 2)
+        finish_aside(0, 0)
+        sigmoid(1, 0, 2, 0, 2)
+        sigmoid(1, 0, 2, 2, 4)
+        finish(1, 1)
+        store(0, 1, 2, 2, 4)
+        finish(1, 0)
         recip(2)
         recip(3)
-        finish(1, 1)
-        store(0, 1, 2, 0, 4)
+        store(0, 0, 1, 0, 4)
         finish(2, 0)
         store(1, 0, 1, 0, 2)
         recip(4)

@@ -43,7 +43,7 @@ def tile_rows_lin_relu1_norm_gate_kernel(tc, q, qa, ka, k, t, v, og, out):
         warm2 = sb.tile([P, 8], F32, name="warm2", align_bytes=64)
         k_raw = tiles("k_raw", heads, [P, PACK, D], F32)
         k_relu = tiles("k_relu", heads, [P, PACK, R, PACK], F32)
-        k_bf = tiles("k_bf", heads, [P, PACK, R, PACK], BF16)
+        k_bf = tiles("k_bf", pairs, [P, PACK, 2, R, PACK], BF16)
         k_codes = tiles("k_codes", pairs, [P, PACK, 3 * R], U32)
         k_scales = tiles("k_scales", pairs, [P, PACK, 3 * R], U8)
         v_raw = tiles("v_raw", pairs, [P, 2, PACK, E], F32)
@@ -120,13 +120,13 @@ def tile_rows_lin_relu1_norm_gate_kernel(tc, q, qa, ka, k, t, v, og, out):
         def load_og(g):
             nc.sync.dma_start(out=og_raw[g][:].rearrange("p c (u r) e -> p (c u) (r e)", u=2), in_=rows2(og, g))
 
-        def store(g, c0, c1, r0, r1):
+        def store(g, c0, c1, r0, r1, queue=nc.sync):
             dst = rows2(out, g).rearrange("s (c u) x -> s c u x", u=2)
             src = res[g][:].rearrange("p c (u r) e -> p c u (r e)", u=2)
             if r1 - r0 == 4:
-                nc.sync.dma_start(out=dst[:, c0], in_=src[:, c0])
+                queue.dma_start(out=dst[:, c0], in_=src[:, c0])
             else:
-                nc.sync.dma_start(out=dst[:, c0:c1, r0 // 2], in_=src[:, c0:c1, r0 // 2])
+                queue.dma_start(out=dst[:, c0:c1, r0 // 2], in_=src[:, c0:c1, r0 // 2])
 
         def make_tka(m0, m1):
             shape = [P, PACK, m1 - m0, PACK]
@@ -150,15 +150,26 @@ def tile_rows_lin_relu1_norm_gate_kernel(tc, q, qa, ka, k, t, v, og, out):
 
         def scale_k(h, m0=0, m1=R):
             nc.vector.scalar_tensor_tensor(
-                out=k_bf[h][:, :, m0:m1, :], in0=k_relu[h][:, :, m0:m1, :], scalar=PHI,
+                out=k_bf[h // 2][:, :, h % 2, m0:m1, :], in0=k_relu[h][:, :, m0:m1, :], scalar=PHI,
                 in1=tka[:, :, m0:m1, :], op0=ALU.add, op1=ALU.mult)
 
-        def quant_k(h):
+        def quant_k_head(h):
             g, c = divmod(h, 2)
             cols = slice(2 * R * c, 2 * R * c + R)
             for x in range(PACK):
                 nc.vector.quantize_mx(out=k_codes[g][:, x, cols].bitcast(FP8X4), scales=k_scales[g][:, x, cols],
-                                      in_=k_bf[h][:, x].rearrange("p m j -> p (m j)"))
+                                      in_=k_bf[g][:, x, c].rearrange("p m j -> p (m j)"))
+
+        def quant_k(g):
+            src = k_bf[g][:].rearrange("p x c m j -> p (x c m j)")
+            codes = k_codes[g][:].rearrange("p x w -> p (x w)")
+            scales = k_scales[g][:].rearrange("p x w -> p (x w)")
+            for x in range(PACK + 1):
+                n0, n1 = max(2 * x - 1, 0), min(2 * x + 1, 2 * PACK)
+                w0 = max(3 * x - 1, 0) * R
+                cols = slice(w0, w0 + (n1 - n0) * R)
+                nc.vector.quantize_mx(out=codes[:, cols].bitcast(FP8X4), scales=scales[:, cols],
+                                      in_=src[:, n0 * D:n1 * D])
 
         def v_views(h):
             g, c = divmod(h, 2)
@@ -327,36 +338,39 @@ def tile_rows_lin_relu1_norm_gate_kernel(tc, q, qa, ka, k, t, v, og, out):
         q_consts_b()
         relu_k(1, 0, 32)
         relu_k(1, 32, 64)
-        quant_k(0)
+        quant_k_head(0)
         scale_k(1, 0, 32)
         scale_k(1, 32, 64)
-        relu_k(2, 0, 64)
+        relu_k(2, 0, 32)
+        relu_k(2, 32, 64)
         cast_v(0)
         cast_v(1)
-        quant_k(1)
-        scale_k(2, 0, 64)
+        scale_k(2, 0, 32)
+        quant_k_head(1)
+        scale_k(2, 32, 64)
         quant_v(0)
         mm_state(0)
-        quant_k(2)
+        quant_k_head(2)
         relu_k(3, 0, 32)
         relu_k(3, 32, 64)
         scale_k(3, 0, 32)
         scale_k(3, 32, 64)
         for j in range(3):
             affine_q(0, j)
+        clamp_q(0, 0)
+        quant_k_head(3)
         affine_q_vector(0, 3)
-        quant_k(3)
-        for j in (0, 1, 3, 2):
+        for j in (1, 2, 3):
             clamp_q(0, j)
         evac_state(0)
         cast_v(2)
         cast_v_vector(3)
-        weave_q_scalar(1, 128, 256)
+        weave_q_scalar(1, 160, 256)
         quant_s(0)
         weave_q(0)
         quant_v(1)
         mm_state(1)
-        weave_q(1, 0, 128)
+        weave_q(1, 0, 160)
         quant_q(0)
         mm_read(0)
         affine_q(1, 0)
@@ -368,16 +382,16 @@ def tile_rows_lin_relu1_norm_gate_kernel(tc, q, qa, ka, k, t, v, og, out):
         quant_q(1)
         mm_read(1)
         evac_state(1)
-        sigmoid(0, 1, 2, 0, 4)
         weave_q_scalar(3, 128, 256)
+        sigmoid(0, 1, 2, 0, 4)
         sigmoid(0, 0, 1, 0, 4)
         weave_q(2)
         quant_s(1)
         weave_q(3, 0, 128)
+        recip(0)
         recip(1)
         quant_q(2)
         mm_read(2)
-        recip(0)
         quant_q(3)
         mm_read(3)
         finish(0, 1)
@@ -385,12 +399,13 @@ def tile_rows_lin_relu1_norm_gate_kernel(tc, q, qa, ka, k, t, v, og, out):
         finish_aside(0, 0)
         sigmoid(1, 0, 2, 0, 2)
         sigmoid(1, 0, 2, 2, 4)
+        store(0, 0, 1, 0, 2, nc.scalar)
         finish(1, 1)
         store(0, 1, 2, 2, 4)
         finish(1, 0)
+        store(0, 0, 1, 2, 4)
         recip(2)
         recip(3)
-        store(0, 0, 1, 0, 4)
         finish(2, 0)
         store(1, 0, 1, 0, 2)
         recip(4)

@@ -17,8 +17,12 @@ ALU = mybir.AluOpType
 P = 128
 R = 64
 PACK = 4
+HALF = N // 2
 PHI = 0.125
 BIG = 3.0e38
+HEAD0_CUTS = (0, 16, 40, R)
+VECTOR_COLUMNS_HALF1 = 160
+VECTOR_COLUMNS_HALF3 = 128
 
 
 def tile_rows_lin_relu1_norm_gate_kernel(tc, q, qa, ka, k, t, v, og, out):
@@ -28,155 +32,106 @@ def tile_rows_lin_relu1_norm_gate_kernel(tc, q, qa, ka, k, t, v, og, out):
         ps = ctx.enter_context(tc.psum_pool(name="ps", bufs=1))
         ctx.enter_context(tc.manual_schedule())
 
-        def tiles(name, keys, shape, dtype):
-            return {key: sb.tile(shape, dtype, name="%s_%s" % (name, key), align_bytes=64) for key in keys}
+        def tile(name, shape, dtype):
+            return sb.tile(shape, dtype, name=name, align_bytes=64)
 
-        heads = range(H)
-        pairs = range(2)
-        halves = range(4)
+        def tiles(name, count, shape, dtype):
+            return [tile("%s_%d" % (name, i), shape, dtype) for i in range(count)]
 
-        t_sb = sb.tile([P, PACK], F32, name="t_sb", align_bytes=64)
-        qa_sb = sb.tile([P, PACK], F32, name="qa_sb", align_bytes=64)
-        ka_sb = sb.tile([P, D], F32, name="ka_sb", align_bytes=64)
-        tka = sb.tile([P, PACK, R, PACK], F32, name="tka", align_bytes=64)
-        warm = sb.tile([P, 8], F32, name="warm", align_bytes=64)
-        warm2 = sb.tile([P, 8], F32, name="warm2", align_bytes=64)
-        k_raw = tiles("k_raw", heads, [P, PACK, D], F32)
-        k_relu = tiles("k_relu", heads, [P, PACK, R, PACK], F32)
-        k_bf = tiles("k_bf", pairs, [P, PACK, 2, R, PACK], BF16)
-        k_codes = tiles("k_codes", pairs, [P, PACK, 3 * R], U32)
-        k_scales = tiles("k_scales", pairs, [P, PACK, 3 * R], U8)
-        v_raw = tiles("v_raw", pairs, [P, 2, PACK, E], F32)
-        v_bf = tiles("v_bf", pairs, [P, 2, E, PACK], BF16)
-        v_codes = tiles("v_codes", pairs, [P, 2 * E], U32)
-        v_scales = tiles("v_scales", pairs, [P, 2 * E], U8)
-        s_bf = tiles("s_bf", pairs, [P, E, PACK], BF16)
-        s_codes = tiles("s_codes", pairs, [P, E], U32)
-        s_scales = tiles("s_scales", pairs, [P, E], U8)
-        BYROW = [1,1]
-        q_raw = {}
-        for half in halves:
-            q_raw[half] = sb.tile([P, 2, N] if BYROW[half // 2] else [P, PACK, N // 2], F32, name="q_raw_%d" % half,
-                                  align_bytes=64)
-        q_aff = tiles("q_aff", pairs, [P, PACK, N], BF16)
-        q_phi = tiles("q_phi", pairs, [P, PACK, N], BF16)
-        qa8 = sb.tile([P, PACK], F32, name="qa8", align_bytes=64)
-        qa_side = sb.tile([P, PACK], F32, name="qa_side", align_bytes=64)
-        q_lo = sb.tile([P, PACK], F32, name="q_lo", align_bytes=64)
-        q_hi = sb.tile([P, PACK], F32, name="q_hi", align_bytes=64)
-        q_bf = tiles("q_bf", halves, [P, 2, P, PACK], BF16)
-        q_codes = tiles("q_codes", halves, [P, 2 * P], U32)
-        q_scales = tiles("q_scales", halves, [P, 2 * P], U8)
-        og_raw = tiles("og_raw", pairs, [P, 2, PACK, E], F32)
-        gate = tiles("gate", pairs, [P, 2, PACK, E], F32)
-        res = tiles("res", pairs, [P, 2, PACK, E], F32)
-        ynorm = tiles("ynorm", pairs, [P, 2, PACK, E], F32)
-        rden = tiles("rden", range(6), [P, 4], F32)
-        s_ps = {g: ps.tile([P, PACK, E], F32, name="s_ps_%d" % g) for g in pairs}
-        y_ps = {b: ps.tile([P, 4, E], F32, name="y_ps_%d" % b) for b in range(6)}
+        t_sb = tile("t_sb", [P, PACK], F32)
+        qa_sb = tile("qa_sb", [P, PACK], F32)
+        ka_sb = tile("ka_sb", [P, D], F32)
+        tka = tile("tka", [P, PACK, R, PACK], F32)
+        table_in = tile("table_in", [P, 8], F32)
+        table_out = tile("table_out", [P, 8], F32)
+        k_raw = tiles("k_raw", H, [P, PACK, D], F32)
+        k_relu = tiles("k_relu", H, [P, PACK, R, PACK], F32)
+        k_bf = tiles("k_bf", H, [P, PACK, R, PACK], BF16)
+        k_codes = tiles("k_codes", 2, [P, PACK, 3 * R], U32)
+        k_scales = tiles("k_scales", 2, [P, PACK, 3 * R], U8)
+        v_raw = tiles("v_raw", 2, [P, 2, PACK, E], F32)
+        v_bf = tiles("v_bf", 2, [P, 2, E, PACK], BF16)
+        v_codes = tiles("v_codes", 2, [P, 2 * E], U32)
+        v_scales = tiles("v_scales", 2, [P, 2 * E], U8)
+        s_bf = tiles("s_bf", 2, [P, E, PACK], BF16)
+        s_codes = tiles("s_codes", 2, [P, E], U32)
+        s_scales = tiles("s_scales", 2, [P, E], U8)
+        q_raw = tiles("q_raw", 4, [P, 2, N], F32)
+        q_aff = tiles("q_aff", 2, [P, PACK, N], BF16)
+        q_phi = tiles("q_phi", 2, [P, PACK, N], BF16)
+        qa8 = tile("qa8", [P, PACK], F32)
+        qa_side = tile("qa_side", [P, PACK], F32)
+        q_lo = tile("q_lo", [P, PACK], F32)
+        q_hi = tile("q_hi", [P, PACK], F32)
+        q_bf = tiles("q_bf", 4, [P, HALF, PACK], BF16)
+        q_codes = tiles("q_codes", 4, [P, HALF], U32)
+        q_scales = tiles("q_scales", 4, [P, HALF], U8)
+        og_raw = tiles("og_raw", 2, [P, 2, 2, 2, E], F32)
+        gate = tiles("gate", 2, [P, 2, 2, 2, E], F32)
+        res = tiles("res", 2, [P, 2, 2, 2, E], F32)
+        y_norm = tile("y_norm", [P, 2, E], F32)
+        rden = tiles("rden", 6, [P, 4], F32)
+        s_ps = [ps.tile([P, PACK, E], F32, name="s_ps_%d" % g) for g in range(2)]
+        y_ps = [ps.tile([P, 4, E], F32, name="y_ps_%d" % b) for b in range(6)]
 
         def y_place(half, c):
             if half < 2:
                 return c, 2 * half
             return 2 * (half - 1) + c, 0
 
-        def init():
-            nc.vector.memset(warm[:], 0.0)
-            nc.scalar.activation(out=warm2[:], in_=warm[:], func=ACT.Sigmoid)
-            for g in pairs:
-                nc.gpsimd.memset(k_codes[g][:, :, R:2 * R], 0)
-                nc.gpsimd.memset(k_scales[g][:].bitcast(I32)[:, :, R // 4:R // 2], 0)
-
-        def load_t():
-            nc.scalar.dma_start(out=t_sb[:], in_=t.rearrange("(p j) o -> p (j o)", j=PACK))
-
-        def load_ka():
-            nc.sync.dma_start(out=ka_sb[:], in_=ka)
-
-        def load_qa():
-            for c in range(2):
-                nc.scalar.dma_start(out=qa_sb[R * c:R * c + R, :], in_=qa.rearrange("(p j) o -> p (j o)", j=PACK))
-
         def load_k(h):
             nc.sync.dma_start(out=k_raw[h][:], in_=k[h].rearrange("(p j) d -> p j d", j=PACK))
 
-        def rows(x, g):
-            return x[2 * g:2 * g + 2].rearrange("c (p j) e -> p c (j e)", j=PACK)
+        def load_v(g):
+            nc.sync.dma_start(out=v_raw[g][:].rearrange("p c j e -> p c (j e)"),
+                              in_=v[2 * g:2 * g + 2].rearrange("c (p j) e -> p c (j e)", j=PACK))
 
-        def rows2(x, g):
+        def load_q(g):
+            src = q[2 * g:2 * g + 2].rearrange("c (m x) n -> (c m) x n", x=PACK)
+            for i in range(2):
+                nc.sync.dma_start(out=q_raw[2 * g + i][:], in_=src[:, 2 * i:2 * i + 2, :])
+
+        def row_pairs(x, g):
             return x[2 * g:2 * g + 2].rearrange("c (u s r) e -> s (c u) (r e)", u=2, r=2)
 
-        def load_v(g):
-            nc.sync.dma_start(out=v_raw[g][:].rearrange("p c j e -> p c (j e)"), in_=rows(v, g))
-
-        def load_q(half):
-            g, u = divmod(half, 2)
-            src = q[2 * g:2 * g + 2].rearrange("c (p j) n -> (c p) j n", j=PACK)
-            if BYROW[g]:
-                nc.sync.dma_start(out=q_raw[half][:], in_=src[:, 2 * u:2 * u + 2, :])
-            else:
-                nc.sync.dma_start(out=q_raw[half][:], in_=src[:, :, 2 * P * u:2 * P * (u + 1)])
-
         def load_og(g):
-            nc.sync.dma_start(out=og_raw[g][:].rearrange("p c (u r) e -> p (c u) (r e)", u=2), in_=rows2(og, g))
+            nc.sync.dma_start(out=og_raw[g][:].rearrange("p c u r e -> p (c u) (r e)"), in_=row_pairs(og, g))
 
-        def store(g, c0, c1, r0, r1, queue=nc.sync):
-            dst = rows2(out, g).rearrange("s (c u) x -> s c u x", u=2)
-            src = res[g][:].rearrange("p c (u r) e -> p c u (r e)", u=2)
-            if r1 - r0 == 4:
-                queue.dma_start(out=dst[:, c0], in_=src[:, c0])
-            else:
-                queue.dma_start(out=dst[:, c0:c1, r0 // 2], in_=src[:, c0:c1, r0 // 2])
-
-        def make_tka(m0, m1):
-            shape = [P, PACK, m1 - m0, PACK]
-            nc.vector.tensor_tensor(
-                out=tka[:, :, m0:m1, :],
-                in0=ka_sb[:, 4 * m0:4 * m1].rearrange("p (m x) -> p x m", x=PACK).unsqueeze(3).to_broadcast(shape),
-                in1=t_sb[:].unsqueeze(1).unsqueeze(1).to_broadcast(shape),
-                op=ALU.mult)
+        def store(half, c, queue):
+            g, u = divmod(half, 2)
+            queue.dma_start(out=row_pairs(out, g)[:, 2 * c + u, :], in_=res[g][:, c, u].rearrange("p r e -> p (r e)"))
 
         def relu_views(h, m0, m1):
             return (k_relu[h][:, :, m0:m1, :].rearrange("p x m j -> p m j x"),
-                    k_raw[h][:, :, 4 * m0:4 * m1].rearrange("p j (m x) -> p m j x", x=PACK))
+                    k_raw[h][:, :, PACK * m0:PACK * m1].rearrange("p j (m x) -> p m j x", x=PACK))
 
-        def relu_k(h, m0=0, m1=R):
+        def relu_k(h, m0, m1):
             dst, src = relu_views(h, m0, m1)
             nc.scalar.activation(out=dst, in_=src, func=ACT.Relu)
 
-        def relu_k_vector(h, m0, m1):
-            dst, src = relu_views(h, m0, m1)
-            nc.vector.tensor_scalar(out=dst, in0=src, scalar1=0.0, scalar2=None, op0=ALU.max)
+        def relu_k_halves(h):
+            relu_k(h, 0, R // 2)
+            relu_k(h, R // 2, R)
 
-        def scale_k(h, m0=0, m1=R):
-            nc.vector.scalar_tensor_tensor(
-                out=k_bf[h // 2][:, :, h % 2, m0:m1, :], in0=k_relu[h][:, :, m0:m1, :], scalar=PHI,
-                in1=tka[:, :, m0:m1, :], op0=ALU.add, op1=ALU.mult)
+        def scale_k(h, m0, m1):
+            nc.vector.scalar_tensor_tensor(out=k_bf[h][:, :, m0:m1, :], in0=k_relu[h][:, :, m0:m1, :], scalar=PHI,
+                                           in1=tka[:, :, m0:m1, :], op0=ALU.add, op1=ALU.mult)
 
-        def quant_k_head(h):
+        def quant_k(h):
             g, c = divmod(h, 2)
             cols = slice(2 * R * c, 2 * R * c + R)
             for x in range(PACK):
                 nc.vector.quantize_mx(out=k_codes[g][:, x, cols].bitcast(FP8X4), scales=k_scales[g][:, x, cols],
-                                      in_=k_bf[g][:, x, c].rearrange("p m j -> p (m j)"))
+                                      in_=k_bf[h][:, x].rearrange("p m j -> p (m j)"))
 
-        def quant_k(g):
-            src = k_bf[g][:].rearrange("p x c m j -> p (x c m j)")
-            codes = k_codes[g][:].rearrange("p x w -> p (x w)")
-            scales = k_scales[g][:].rearrange("p x w -> p (x w)")
-            for x in range(PACK + 1):
-                n0, n1 = max(2 * x - 1, 0), min(2 * x + 1, 2 * PACK)
-                w0 = max(3 * x - 1, 0) * R
-                cols = slice(w0, w0 + (n1 - n0) * R)
-                nc.vector.quantize_mx(out=codes[:, cols].bitcast(FP8X4), scales=scales[:, cols],
-                                      in_=src[:, n0 * D:n1 * D])
+        def interleave_views(dst, src):
+            return dst.rearrange("p (b i) j -> p b j i", i=4), src.rearrange("p j (b i) -> p b j i", i=4)
 
         def v_views(h):
             g, c = divmod(h, 2)
-            return (v_bf[g][:, c].rearrange("p (b i) j -> p b j i", i=4),
-                    v_raw[g][:, c].rearrange("p j (b i) -> p b j i", i=4))
+            return interleave_views(v_bf[g][:, c], v_raw[g][:, c])
 
-        def cast_v(h):
+        def cast_v_scalar(h):
             dst, src = v_views(h)
             nc.scalar.copy(out=dst, in_=src)
 
@@ -197,222 +152,181 @@ def tile_rows_lin_relu1_norm_gate_kernel(tc, q, qa, ka, k, t, v, og, out):
                                         lhsT_scale=k_scales[g][:, x, cols], rhs=v_codes[g][:, vc].bitcast(FP8X4),
                                         rhs_scale=v_scales[g][:, vc], start=(c == 0), stop=(c == 1))
 
-        def evac_state(g):
+        def read_state(g):
             nc.scalar.activation(out=s_bf[g][:], in_=s_ps[g][:].rearrange("p x e -> p e x"), func=ACT.Copy,
                                  scale=1.0 / N)
-
-        def evac_state_vector(g):
-            nc.vector.tensor_scalar(out=s_bf[g][:], in0=s_ps[g][:].rearrange("p x e -> p e x"), scalar1=1.0 / N,
-                                    scalar2=None, op0=ALU.mult)
 
         def quant_s(g):
             nc.vector.quantize_mx(out=s_codes[g][:].bitcast(FP8X4), scales=s_scales[g][:],
                                   in_=s_bf[g][:].rearrange("p e x -> p (e x)"))
 
-        def q_consts_a():
-            nc.vector.tensor_scalar(out=qa8[:], in0=qa_sb[:], scalar1=PHI, scalar2=None, op0=ALU.mult)
-            nc.vector.tensor_scalar(out=qa_side[:], in0=qa_sb[:], scalar1=0.0, scalar2=0.5, op0=ALU.is_ge,
-                                    op1=ALU.subtract)
+        def affine_views(g, x):
+            return (q_aff[g][:, x, :].rearrange("p (u r s) -> p u r s", u=2, r=2),
+                    q_raw[2 * g + x // 2][:, x % 2, :].rearrange("p (u s r) -> p u r s", u=2, r=2))
 
-        def q_consts_b():
-            nc.vector.scalar_tensor_tensor(out=q_lo[:], in0=qa_side[:], scalar=BIG, in1=qa8[:], op0=ALU.mult,
-                                           op1=ALU.min)
-            nc.vector.scalar_tensor_tensor(out=q_hi[:], in0=qa_side[:], scalar=BIG, in1=qa8[:], op0=ALU.mult,
-                                           op1=ALU.max)
+        def affine_q_scalar(g, x):
+            dst, src = affine_views(g, x)
+            nc.scalar.activation(out=dst, in_=src, func=ACT.Identity, scale=qa_sb[:, x:x + 1], bias=qa8[:, x:x + 1])
 
-        def affine_views(g, j, u):
-            if BYROW[g]:
-                return (q_aff[g][:, j, :].rearrange("p (u r s) -> p u r s", u=2, r=2),
-                        q_raw[2 * g + j // 2][:, j % 2, :].rearrange("p (u s r) -> p u r s", u=2, r=2))
-            return (q_aff[g][:, j, 2 * P * u:2 * P * (u + 1)].rearrange("p (r s) -> p r s", r=2),
-                    q_raw[2 * g + u][:, j, :].rearrange("p (s r) -> p r s", r=2))
-
-        def affine_q(g, j, u=0):
-            dst, src = affine_views(g, j, u)
-            nc.scalar.activation(out=dst, in_=src, func=ACT.Identity, scale=qa_sb[:, j:j + 1], bias=qa8[:, j:j + 1])
-
-        def affine_q_vector(g, j, u=0):
-            dst, src = affine_views(g, j, u)
-            nc.vector.tensor_scalar(out=dst, in0=src, scalar1=qa_sb[:, j:j + 1], scalar2=qa8[:, j:j + 1],
+        def affine_q_vector(g, x):
+            dst, src = affine_views(g, x)
+            nc.vector.tensor_scalar(out=dst, in0=src, scalar1=qa_sb[:, x:x + 1], scalar2=qa8[:, x:x + 1],
                                     op0=ALU.mult, op1=ALU.add)
 
-        def affine_q_gpsimd(g, j, u=0):
-            dst, src = affine_views(g, j, u)
-            nc.gpsimd.tensor_scalar(out=dst, in0=src, scalar1=qa_sb[:, j:j + 1], scalar2=qa8[:, j:j + 1],
-                                    op0=ALU.mult, op1=ALU.add)
+        def clamp_q(g, x):
+            nc.vector.tensor_scalar(out=q_phi[g][:, x, :], in0=q_aff[g][:, x, :], scalar1=q_lo[:, x:x + 1],
+                                    scalar2=q_hi[:, x:x + 1], op0=ALU.max, op1=ALU.min)
 
-        def clamp_q(g, j, u=0):
-            cols = slice(0, N) if BYROW[g] else slice(2 * P * u, 2 * P * (u + 1))
-            nc.vector.tensor_scalar(out=q_phi[g][:, j, cols], in0=q_aff[g][:, j, cols], scalar1=q_lo[:, j:j + 1],
-                                    scalar2=q_hi[:, j:j + 1], op0=ALU.max, op1=ALU.min)
-
-        def weave_views(half, n0, n1):
+        def q_views(half, n0, n1):
             g, u = divmod(half, 2)
-            src = q_phi[g][:, :, 2 * P * u + n0:2 * P * u + n1].rearrange("p j (b i) -> p b j i", i=4)
-            dst = q_bf[half][:].rearrange("p r s j -> p (r s) j")[:, n0:n1, :]
-            return dst.rearrange("p (b i) j -> p b j i", i=4), src
+            return interleave_views(q_bf[half][:, n0:n1, :], q_phi[g][:, :, HALF * u + n0:HALF * u + n1])
 
-        def weave_q(half, n0=0, n1=2 * P):
-            dst, src = weave_views(half, n0, n1)
+        def interleave_q_vector(half, n0, n1):
+            dst, src = q_views(half, n0, n1)
             nc.vector.tensor_copy(out=dst, in_=src)
 
-        def weave_q_scalar(half, n0=0, n1=2 * P):
-            dst, src = weave_views(half, n0, n1)
+        def interleave_q_scalar(half, n0, n1):
+            dst, src = q_views(half, n0, n1)
             nc.scalar.copy(out=dst, in_=src)
-
-        def weave_q_gpsimd(half, n0=0, n1=2 * P):
-            dst, src = weave_views(half, n0, n1)
-            nc.gpsimd.tensor_scalar(out=dst, in0=src, scalar1=1.0, scalar2=0.0, op0=ALU.mult, op1=ALU.add)
 
         def quant_q(half):
             nc.vector.quantize_mx(out=q_codes[half][:].bitcast(FP8X4), scales=q_scales[half][:],
-                                  in_=q_bf[half][:].rearrange("p r n j -> p (r n j)"))
+                                  in_=q_bf[half][:].rearrange("p n x -> p (n x)"))
 
         def mm_read(half):
             g = half // 2
             for c in range(2):
+                bank, slot = y_place(half, c)
+                part = slice(R * c, R * c + R)
                 for r in range(2):
-                    b, slot = y_place(half, c)
-                    part = slice(R * c, R * c + R)
                     cols = slice(P * r, P * r + P)
-                    nc.tensor.matmul_mx(out=y_ps[b][:, slot + r, :], lhsT=q_codes[half][part, cols].bitcast(FP8X4),
+                    nc.tensor.matmul_mx(out=y_ps[bank][:, slot + r, :],
+                                        lhsT=q_codes[half][part, cols].bitcast(FP8X4),
                                         lhsT_scale=q_scales[half][part, cols], rhs=s_codes[g][part, :].bitcast(FP8X4),
                                         rhs_scale=s_scales[g][part, :], start=True, stop=True)
 
-        def sigmoid(g, c0, c1, r0, r1):
-            nc.scalar.activation(out=gate[g][:, c0:c1, r0:r1, :], in_=og_raw[g][:, c0:c1, r0:r1, :], func=ACT.Sigmoid)
+        def recip(bank, slots):
+            nc.vector.reciprocal(out=rden[bank][:, 0:slots], in_=y_ps[bank][:, 0:slots, E - 1])
 
-        def recip(b):
-            n = 4 if b < 2 else 2
-            nc.vector.reciprocal(out=rden[b][:, 0:n], in_=y_ps[b][:, 0:n, E - 1])
-
-        def finish(half, c):
+        def finish(half, c, rows=(0, 1)):
             g, u = divmod(half, 2)
-            b, slot = y_place(half, c)
-            for r in range(2):
-                nc.vector.scalar_tensor_tensor(
-                    out=res[g][:, c, 2 * u + r, :], in0=y_ps[b][:, slot + r, :],
-                    scalar=rden[b][:, slot + r:slot + r + 1],
-                    in1=gate[g][:, c, 2 * u + r, :], op0=ALU.mult, op1=ALU.mult)
+            bank, slot = y_place(half, c)
+            for r in rows:
+                nc.vector.scalar_tensor_tensor(out=res[g][:, c, u, r, :], in0=y_ps[bank][:, slot + r, :],
+                                               scalar=rden[bank][:, slot + r:slot + r + 1],
+                                               in1=gate[g][:, c, u, r, :], op0=ALU.mult, op1=ALU.mult)
 
-        def normalise(half, c):
-            g, u = divmod(half, 2)
-            b, slot = y_place(half, c)
-            for r in range(2):
-                nc.scalar.activation(out=ynorm[g][:, c, 2 * u + r, :], in_=y_ps[b][:, slot + r, :], func=ACT.Copy,
-                                     scale=rden[b][:, slot + r:slot + r + 1])
-
-        def gate_gpsimd(half, c):
-            g, u = divmod(half, 2)
-            nc.gpsimd.tensor_tensor(out=res[g][:, c, 2 * u:2 * u + 2, :], in0=ynorm[g][:, c, 2 * u:2 * u + 2, :],
-                                    in1=gate[g][:, c, 2 * u:2 * u + 2, :], op=ALU.mult)
-
-        def finish_aside(half, c):
-            normalise(half, c)
-            gate_gpsimd(half, c)
-
-        load_t()
-        load_qa()
-        init()
-        load_ka()
-        load_k(0)
-        load_k(1)
-        load_k(2)
+        nc.scalar.dma_start(out=t_sb[:], in_=t.rearrange("(p j) o -> p (j o)", j=PACK))
+        for c in range(2):
+            nc.scalar.dma_start(out=qa_sb[R * c:R * c + R, :], in_=qa.rearrange("(m x) o -> m (x o)", x=PACK))
+        nc.vector.memset(table_in[:], 0.0)
+        nc.scalar.activation(out=table_out[:], in_=table_in[:], func=ACT.Sigmoid)
+        for g in range(2):
+            nc.gpsimd.memset(k_codes[g][:, :, R:2 * R], 0)
+            nc.gpsimd.memset(k_scales[g][:].bitcast(I32)[:, :, R // 4:R // 2], 0)
+        nc.sync.dma_start(out=ka_sb[:], in_=ka)
+        for h in range(3):
+            load_k(h)
         load_v(0)
         load_k(3)
         load_q(0)
-        load_q(1)
         load_v(1)
-        load_q(2)
-        load_q(3)
+        load_q(1)
         load_og(0)
         load_og(1)
-        make_tka(0, R)
-        relu_k_vector(0, 0, 16)
-        q_consts_a()
-        relu_k(0, 16, 40)
-        relu_k(0, 40, 64)
-        scale_k(0, 0, 16)
-        scale_k(0, 16, 40)
-        scale_k(0, 40, 64)
-        q_consts_b()
-        relu_k(1, 0, 32)
-        relu_k(1, 32, 64)
-        quant_k_head(0)
-        scale_k(1, 0, 32)
-        scale_k(1, 32, 64)
-        relu_k(2, 0, 32)
-        relu_k(2, 32, 64)
-        cast_v(0)
-        cast_v(1)
-        scale_k(2, 0, 32)
-        quant_k_head(1)
-        scale_k(2, 32, 64)
+
+        shape = [P, PACK, R, PACK]
+        nc.vector.tensor_tensor(out=tka[:], in0=ka_sb[:].rearrange("p (m x) -> p x m", x=PACK).unsqueeze(3).to_broadcast(shape),
+                                in1=t_sb[:].unsqueeze(1).unsqueeze(1).to_broadcast(shape), op=ALU.mult)
+        dst, src = relu_views(0, HEAD0_CUTS[0], HEAD0_CUTS[1])
+        nc.vector.tensor_scalar(out=dst, in0=src, scalar1=0.0, scalar2=None, op0=ALU.max)
+        nc.vector.tensor_scalar(out=qa8[:], in0=qa_sb[:], scalar1=PHI, scalar2=None, op0=ALU.mult)
+        nc.vector.tensor_scalar(out=qa_side[:], in0=qa_sb[:], scalar1=0.0, scalar2=0.5, op0=ALU.is_ge,
+                                op1=ALU.subtract)
+        for i in (1, 2):
+            relu_k(0, HEAD0_CUTS[i], HEAD0_CUTS[i + 1])
+        for i in range(3):
+            scale_k(0, HEAD0_CUTS[i], HEAD0_CUTS[i + 1])
+        nc.vector.scalar_tensor_tensor(out=q_lo[:], in0=qa_side[:], scalar=BIG, in1=qa8[:], op0=ALU.mult, op1=ALU.min)
+        nc.vector.scalar_tensor_tensor(out=q_hi[:], in0=qa_side[:], scalar=BIG, in1=qa8[:], op0=ALU.mult, op1=ALU.max)
+        quant_k(0)
+        relu_k_halves(1)
+        scale_k(1, 0, R // 2)
+        scale_k(1, R // 2, R)
+        relu_k_halves(2)
+        cast_v_scalar(0)
+        cast_v_scalar(1)
+        scale_k(2, 0, R // 2)
+        quant_k(1)
+        scale_k(2, R // 2, R)
         quant_v(0)
         mm_state(0)
-        quant_k_head(2)
-        relu_k(3, 0, 32)
-        relu_k(3, 32, 64)
-        scale_k(3, 0, 32)
-        scale_k(3, 32, 64)
-        for j in range(3):
-            affine_q(0, j)
+        quant_k(2)
+        relu_k_halves(3)
+        scale_k(3, 0, R // 2)
+        scale_k(3, R // 2, R)
+
+        for x in range(3):
+            affine_q_scalar(0, x)
         clamp_q(0, 0)
-        quant_k_head(3)
+        quant_k(3)
         affine_q_vector(0, 3)
-        for j in (1, 2, 3):
-            clamp_q(0, j)
-        evac_state(0)
-        cast_v(2)
+        for x in range(1, PACK):
+            clamp_q(0, x)
+        read_state(0)
+        cast_v_scalar(2)
         cast_v_vector(3)
-        weave_q_scalar(1, 160, 256)
+        interleave_q_scalar(1, VECTOR_COLUMNS_HALF1, HALF)
         quant_s(0)
-        weave_q(0)
+        interleave_q_vector(0, 0, HALF)
         quant_v(1)
         mm_state(1)
-        weave_q(1, 0, 160)
+        interleave_q_vector(1, 0, VECTOR_COLUMNS_HALF1)
         quant_q(0)
         mm_read(0)
-        affine_q(1, 0)
-        affine_q(1, 1)
-        affine_q(1, 2)
+
+        for x in range(3):
+            affine_q_scalar(1, x)
         affine_q_vector(1, 3)
-        for j in (0, 1, 3, 2):
-            clamp_q(1, j)
+        for x in (0, 1, 3, 2):
+            clamp_q(1, x)
         quant_q(1)
         mm_read(1)
-        evac_state(1)
-        weave_q_scalar(3, 128, 256)
-        sigmoid(0, 1, 2, 0, 4)
-        sigmoid(0, 0, 1, 0, 4)
-        weave_q(2)
+        read_state(1)
+        interleave_q_scalar(3, VECTOR_COLUMNS_HALF3, HALF)
+        for c in (1, 0):
+            nc.scalar.activation(out=gate[0][:, c], in_=og_raw[0][:, c], func=ACT.Sigmoid)
+        interleave_q_vector(2, 0, HALF)
         quant_s(1)
-        weave_q(3, 0, 128)
-        recip(0)
-        recip(1)
-        quant_q(2)
-        mm_read(2)
-        quant_q(3)
-        mm_read(3)
+        interleave_q_vector(3, 0, VECTOR_COLUMNS_HALF3)
+        recip(0, 4)
+        recip(1, 4)
+        for half in (2, 3):
+            quant_q(half)
+            mm_read(half)
+
         finish(0, 1)
-        store(0, 1, 2, 0, 2)
-        finish_aside(0, 0)
-        sigmoid(1, 0, 2, 0, 2)
-        sigmoid(1, 0, 2, 2, 4)
-        store(0, 0, 1, 0, 2, nc.scalar)
+        store(0, 1, nc.sync)
+        for r in range(2):
+            nc.scalar.activation(out=y_norm[:, r, :], in_=y_ps[0][:, r, :], func=ACT.Copy, scale=rden[0][:, r:r + 1])
+        nc.gpsimd.tensor_tensor(out=res[0][:, 0, 0], in0=y_norm[:], in1=gate[0][:, 0, 0], op=ALU.mult)
+        for u in range(2):
+            nc.scalar.activation(out=gate[1][:, :, u], in_=og_raw[1][:, :, u], func=ACT.Sigmoid)
+        store(0, 0, nc.scalar)
         finish(1, 1)
-        store(0, 1, 2, 2, 4)
-        finish(1, 0)
-        store(0, 0, 1, 2, 4)
-        recip(2)
-        recip(3)
+        store(1, 1, nc.sync)
+        finish(1, 0, (0,))
+        recip(2, 2)
+        recip(3, 2)
+        finish(1, 0, (1,))
+        store(1, 0, nc.sync)
         finish(2, 0)
-        store(1, 0, 1, 0, 2)
-        recip(4)
-        recip(5)
+        store(2, 0, nc.scalar)
+        recip(4, 2)
+        recip(5, 2)
         finish(2, 1)
-        store(1, 1, 2, 0, 2)
+        store(2, 1, nc.sync)
         finish(3, 0)
-        store(1, 0, 1, 2, 4)
+        store(3, 0, nc.scalar)
         finish(3, 1)
-        store(1, 1, 2, 2, 4)
+        store(3, 1, nc.sync)

@@ -21,7 +21,7 @@ HALF = N // 2
 PHI = 0.125
 BIG = 3.0e38
 HEAD0_CUTS = (0, 16, 40, R)
-VECTOR_COLUMNS_HALF1 = 160
+VECTOR_COLUMNS_HALF0 = 160
 VECTOR_COLUMNS_HALF3 = 128
 
 
@@ -195,11 +195,11 @@ def tile_rows_lin_relu1_norm_gate_kernel(tc, q, qa, ka, k, t, v, og, out):
 
         def mm_read(half):
             g = half // 2
-            for c in range(2):
-                bank, slot = y_place(half, c)
-                part = slice(R * c, R * c + R)
-                for r in range(2):
-                    cols = slice(P * r, P * r + P)
+            for r in range(2):
+                cols = slice(P * r, P * r + P)
+                for c in range(2):
+                    bank, slot = y_place(half, c)
+                    part = slice(R * c, R * c + R)
                     nc.tensor.matmul_mx(out=y_ps[bank][:, slot + r, :],
                                         lhsT=q_codes[half][part, cols].bitcast(FP8X4),
                                         lhsT_scale=q_scales[half][part, cols], rhs=s_codes[g][part, :].bitcast(FP8X4),
@@ -276,12 +276,12 @@ def tile_rows_lin_relu1_norm_gate_kernel(tc, q, qa, ka, k, t, v, og, out):
         read_state(0)
         cast_v_scalar(2)
         cast_v_vector(3)
-        interleave_q_scalar(1, VECTOR_COLUMNS_HALF1, HALF)
         quant_s(0)
-        interleave_q_vector(0, 0, HALF)
+        interleave_q_scalar(0, VECTOR_COLUMNS_HALF0, HALF)
+        interleave_q_vector(0, 0, VECTOR_COLUMNS_HALF0)
         quant_v(1)
         mm_state(1)
-        interleave_q_vector(1, 0, VECTOR_COLUMNS_HALF1)
+        interleave_q_vector(1, 0, HALF)
         quant_q(0)
         mm_read(0)
 

@@ -46,7 +46,7 @@ def tile_rows_lin_relu1_norm_gate_kernel(tc, q, qa, ka, k, t, v, og, out):
         table_out = tile("table_out", [P, 8], F32)
         k_raw = tiles("k_raw", H, [P, PACK, D], F32)
         k_relu = tiles("k_relu", H, [P, PACK, R, PACK], F32)
-        k_bf = tiles("k_bf", H, [P, PACK, R, PACK], BF16)
+        k_bf = tiles("k_bf", 2, [P, PACK, 2, R, PACK], BF16)
         k_codes = tiles("k_codes", 2, [P, PACK, 3 * R], U32)
         k_scales = tiles("k_scales", 2, [P, PACK, 3 * R], U8)
         v_raw = tiles("v_raw", 2, [P, 2, PACK, E], F32)
@@ -114,7 +114,7 @@ def tile_rows_lin_relu1_norm_gate_kernel(tc, q, qa, ka, k, t, v, og, out):
             relu_k(h, R // 2, R)
 
         def scale_k(h, m0, m1):
-            nc.vector.scalar_tensor_tensor(out=k_bf[h][:, :, m0:m1, :], in0=k_relu[h][:, :, m0:m1, :], scalar=PHI,
+            nc.vector.scalar_tensor_tensor(out=k_bf[h // 2][:, :, h % 2, m0:m1, :], in0=k_relu[h][:, :, m0:m1, :], scalar=PHI,
                                            in1=tka[:, :, m0:m1, :], op0=ALU.add, op1=ALU.mult)
 
         def quant_k(h):
@@ -122,7 +122,18 @@ def tile_rows_lin_relu1_norm_gate_kernel(tc, q, qa, ka, k, t, v, og, out):
             cols = slice(2 * R * c, 2 * R * c + R)
             for x in range(PACK):
                 nc.vector.quantize_mx(out=k_codes[g][:, x, cols].bitcast(FP8X4), scales=k_scales[g][:, x, cols],
-                                      in_=k_bf[h][:, x].rearrange("p m j -> p (m j)"))
+                                      in_=k_bf[g][:, x, c].rearrange("p m j -> p (m j)"))
+
+        def quant_k_pair(g):
+            src = k_bf[g][:].rearrange("p x c m j -> p (x c m j)")
+            codes = k_codes[g][:].rearrange("p x w -> p (x w)")
+            scales = k_scales[g][:].rearrange("p x w -> p (x w)")
+            for x in range(PACK + 1):
+                n0, n1 = max(2 * x - 1, 0), min(2 * x + 1, 2 * PACK)
+                w0 = max(3 * x - 1, 0) * R
+                cols = slice(w0, w0 + (n1 - n0) * R)
+                nc.vector.quantize_mx(out=codes[:, cols].bitcast(FP8X4), scales=scales[:, cols],
+                                      in_=src[:, n0 * D:n1 * D])
 
         def interleave_views(dst, src):
             return dst.rearrange("p (b i) j -> p b j i", i=4), src.rearrange("p j (b i) -> p b j i", i=4)
@@ -261,7 +272,6 @@ def tile_rows_lin_relu1_norm_gate_kernel(tc, q, qa, ka, k, t, v, og, out):
         scale_k(2, R // 2, R)
         quant_v(0)
         mm_state(0)
-        quant_k(2)
         relu_k_halves(3)
         scale_k(3, 0, R // 2)
         scale_k(3, R // 2, R)
@@ -269,7 +279,7 @@ def tile_rows_lin_relu1_norm_gate_kernel(tc, q, qa, ka, k, t, v, og, out):
         for x in range(3):
             affine_q_scalar(0, x)
         clamp_q(0, 0)
-        quant_k(3)
+        quant_k_pair(1)
         affine_q_vector(0, 3)
         for x in range(1, PACK):
             clamp_q(0, x)

@@ -20,9 +20,9 @@ PACK = 4
 HALF = N // 2
 PHI = 0.125
 BIG = 3.0e38
-HEAD0_CUTS = (0, 16, 40, R)
-VECTOR_COLUMNS_HALF0 = 160
-VECTOR_COLUMNS_HALF3 = 128
+HEAD0_PIECES = ((0, 0, 32), (0, 32, R), (1, 0, R))
+VECTOR_COLUMNS_HALF0 = 80
+VECTOR_COLUMNS_HALF3 = 64
 
 
 def tile_rows_lin_relu1_norm_gate_kernel(tc, q, qa, ka, k, t, v, og, out):
@@ -101,21 +101,22 @@ def tile_rows_lin_relu1_norm_gate_kernel(tc, q, qa, ka, k, t, v, og, out):
             g, u = divmod(half, 2)
             queue.dma_start(out=row_pairs(out, g)[:, 2 * c + u, :], in_=res[g][:, c, u].rearrange("p r e -> p (r e)"))
 
-        def relu_views(h, m0, m1):
-            return (k_relu[h][:, :, m0:m1, :].rearrange("p x m j -> p m j x"),
-                    k_raw[h][:, :, PACK * m0:PACK * m1].rearrange("p j (m x) -> p m j x", x=PACK))
+        def relu_views(h, y, m0, m1):
+            return (k_relu[h][:, 2 * y:2 * y + 2, m0:m1, :].rearrange("p x m j -> p m j x"),
+                    k_raw[h][:].rearrange("p j (m x) -> p m j x", x=PACK)[:, m0:m1, :, 2 * y:2 * y + 2])
 
-        def relu_k(h, m0, m1):
-            dst, src = relu_views(h, m0, m1)
+        def relu_k(h, y, m0=0, m1=R):
+            dst, src = relu_views(h, y, m0, m1)
             nc.scalar.activation(out=dst, in_=src, func=ACT.Relu)
 
         def relu_k_halves(h):
-            relu_k(h, 0, R // 2)
-            relu_k(h, R // 2, R)
+            relu_k(h, 0)
+            relu_k(h, 1)
 
-        def scale_k(h, m0, m1):
-            nc.vector.scalar_tensor_tensor(out=k_bf[h // 2][:, :, h % 2, m0:m1, :], in0=k_relu[h][:, :, m0:m1, :], scalar=PHI,
-                                           in1=tka[:, :, m0:m1, :], op0=ALU.add, op1=ALU.mult)
+        def scale_k(h, y, m0=0, m1=R):
+            xs = slice(2 * y, 2 * y + 2)
+            nc.vector.scalar_tensor_tensor(out=k_bf[h // 2][:, xs, h % 2, m0:m1, :], in0=k_relu[h][:, xs, m0:m1, :], scalar=PHI,
+                                           in1=tka[:, xs, m0:m1, :], op0=ALU.add, op1=ALU.mult)
 
         def quant_k(h):
             g, c = divmod(h, 2)
@@ -172,8 +173,7 @@ def tile_rows_lin_relu1_norm_gate_kernel(tc, q, qa, ka, k, t, v, og, out):
                                   in_=s_bf[g][:].rearrange("p e x -> p (e x)"))
 
         def affine_views(g, x):
-            return (q_aff[g][:, x, :].rearrange("p (u r s) -> p u r s", u=2, r=2),
-                    q_raw[2 * g + x // 2][:, x % 2, :].rearrange("p (u s r) -> p u r s", u=2, r=2))
+            return q_aff[g][:, x, :], q_raw[2 * g + x // 2][:, x % 2, :]
 
         def affine_q_scalar(g, x):
             dst, src = affine_views(g, x)
@@ -188,9 +188,11 @@ def tile_rows_lin_relu1_norm_gate_kernel(tc, q, qa, ka, k, t, v, og, out):
             nc.vector.tensor_scalar(out=q_phi[g][:, x, :], in0=q_aff[g][:, x, :], scalar1=q_lo[:, x:x + 1],
                                     scalar2=q_hi[:, x:x + 1], op0=ALU.max, op1=ALU.min)
 
-        def q_views(half, n0, n1):
+        def q_views(half, s0, s1):
             g, u = divmod(half, 2)
-            return interleave_views(q_bf[half][:, n0:n1, :], q_phi[g][:, :, HALF * u + n0:HALF * u + n1])
+            dst = q_bf[half][:].rearrange("p (r s) x -> p s r x", r=2)[:, s0:s1]
+            src = q_phi[g][:, :, HALF * u + 2 * s0:HALF * u + 2 * s1]
+            return dst.rearrange("p (b i) r x -> p b x i r", i=2), src.rearrange("p x (b i r) -> p b x i r", i=2, r=2)
 
         def interleave_q_vector(half, n0, n1):
             dst, src = q_views(half, n0, n1)
@@ -249,32 +251,32 @@ def tile_rows_lin_relu1_norm_gate_kernel(tc, q, qa, ka, k, t, v, og, out):
         shape = [P, PACK, R, PACK]
         nc.vector.tensor_tensor(out=tka[:], in0=ka_sb[:].rearrange("p (m x) -> p x m", x=PACK).unsqueeze(3).to_broadcast(shape),
                                 in1=t_sb[:].unsqueeze(1).unsqueeze(1).to_broadcast(shape), op=ALU.mult)
-        dst, src = relu_views(0, HEAD0_CUTS[0], HEAD0_CUTS[1])
+        dst, src = relu_views(0, *HEAD0_PIECES[0])
         nc.vector.tensor_scalar(out=dst, in0=src, scalar1=0.0, scalar2=None, op0=ALU.max)
         nc.vector.tensor_scalar(out=qa8[:], in0=qa_sb[:], scalar1=PHI, scalar2=None, op0=ALU.mult)
         nc.vector.tensor_scalar(out=qa_side[:], in0=qa_sb[:], scalar1=0.0, scalar2=0.5, op0=ALU.is_ge,
                                 op1=ALU.subtract)
-        for i in (1, 2):
-            relu_k(0, HEAD0_CUTS[i], HEAD0_CUTS[i + 1])
-        for i in range(3):
-            scale_k(0, HEAD0_CUTS[i], HEAD0_CUTS[i + 1])
+        for piece in HEAD0_PIECES[1:]:
+            relu_k(0, *piece)
+        for piece in HEAD0_PIECES:
+            scale_k(0, *piece)
         nc.vector.scalar_tensor_tensor(out=q_lo[:], in0=qa_side[:], scalar=BIG, in1=qa8[:], op0=ALU.mult, op1=ALU.min)
         nc.vector.scalar_tensor_tensor(out=q_hi[:], in0=qa_side[:], scalar=BIG, in1=qa8[:], op0=ALU.mult, op1=ALU.max)
         quant_k(0)
         relu_k_halves(1)
-        scale_k(1, 0, R // 2)
-        scale_k(1, R // 2, R)
+        scale_k(1, 0)
+        scale_k(1, 1)
         relu_k_halves(2)
         cast_v_scalar(0)
         cast_v_scalar(1)
-        scale_k(2, 0, R // 2)
+        scale_k(2, 0)
         quant_k(1)
-        scale_k(2, R // 2, R)
+        scale_k(2, 1)
         quant_v(0)
         mm_state(0)
         relu_k_halves(3)
-        scale_k(3, 0, R // 2)
-        scale_k(3, R // 2, R)
+        scale_k(3, 0)
+        scale_k(3, 1)
 
         for x in range(3):
             affine_q_scalar(0, x)
@@ -287,11 +289,11 @@ def tile_rows_lin_relu1_norm_gate_kernel(tc, q, qa, ka, k, t, v, og, out):
         cast_v_scalar(2)
         cast_v_vector(3)
         quant_s(0)
-        interleave_q_scalar(0, VECTOR_COLUMNS_HALF0, HALF)
+        interleave_q_scalar(0, VECTOR_COLUMNS_HALF0, P)
         interleave_q_vector(0, 0, VECTOR_COLUMNS_HALF0)
         quant_v(1)
         mm_state(1)
-        interleave_q_vector(1, 0, HALF)
+        interleave_q_vector(1, 0, P)
         quant_q(0)
         mm_read(0)
 
@@ -303,10 +305,10 @@ def tile_rows_lin_relu1_norm_gate_kernel(tc, q, qa, ka, k, t, v, og, out):
         quant_q(1)
         mm_read(1)
         read_state(1)
-        interleave_q_scalar(3, VECTOR_COLUMNS_HALF3, HALF)
+        interleave_q_scalar(3, VECTOR_COLUMNS_HALF3, P)
         for c in (1, 0):
             nc.scalar.activation(out=gate[0][:, c], in_=og_raw[0][:, c], func=ACT.Sigmoid)
-        interleave_q_vector(2, 0, HALF)
+        interleave_q_vector(2, 0, P)
         quant_s(1)
         interleave_q_vector(3, 0, VECTOR_COLUMNS_HALF3)
         recip(0, 4)

@@ -19,7 +19,6 @@ R = 64
 PACK = 4
 HALF = N // 2
 PHI = 0.125
-BIG = 3.0e38
 HEAD0_PIECES = ((0, 0, 32), (0, 32, R), (1, 0, R))
 VECTOR_COLUMNS_HALF0 = 80
 VECTOR_COLUMNS_HALF3 = 64
@@ -59,10 +58,9 @@ def tile_rows_lin_relu1_norm_gate_kernel(tc, q, qa, ka, k, t, v, og, out):
         q_raw = tiles("q_raw", 4, [P, 2, N], F32)
         q_aff = tiles("q_aff", 2, [P, PACK, N], BF16)
         q_phi = tiles("q_phi", 2, [P, PACK, N], BF16)
-        qa8 = tile("qa8", [P, PACK], F32)
-        qa_side = tile("qa_side", [P, PACK], F32)
-        q_lo = tile("q_lo", [P, PACK], F32)
-        q_hi = tile("q_hi", [P, PACK], F32)
+        qa_abs = tile("qa_abs", [P, PACK], F32)
+        qa_floor = tile("qa_floor", [P, PACK], F32)
+        qa_sign = tile("qa_sign", [P, PACK], F32)
         q_bf = tiles("q_bf", 4, [P, HALF, PACK], BF16)
         q_codes = tiles("q_codes", 4, [P, HALF], U32)
         q_scales = tiles("q_scales", 4, [P, HALF], U8)
@@ -177,16 +175,16 @@ def tile_rows_lin_relu1_norm_gate_kernel(tc, q, qa, ka, k, t, v, og, out):
 
         def affine_q_scalar(g, x):
             dst, src = affine_views(g, x)
-            nc.scalar.activation(out=dst, in_=src, func=ACT.Identity, scale=qa_sb[:, x:x + 1], bias=qa8[:, x:x + 1])
+            nc.scalar.activation(out=dst, in_=src, func=ACT.Identity, scale=qa_abs[:, x:x + 1], bias=qa_floor[:, x:x + 1])
 
         def affine_q_vector(g, x):
             dst, src = affine_views(g, x)
-            nc.vector.tensor_scalar(out=dst, in0=src, scalar1=qa_sb[:, x:x + 1], scalar2=qa8[:, x:x + 1],
+            nc.vector.tensor_scalar(out=dst, in0=src, scalar1=qa_abs[:, x:x + 1], scalar2=qa_floor[:, x:x + 1],
                                     op0=ALU.mult, op1=ALU.add)
 
         def clamp_q(g, x):
-            nc.vector.tensor_scalar(out=q_phi[g][:, x, :], in0=q_aff[g][:, x, :], scalar1=q_lo[:, x:x + 1],
-                                    scalar2=q_hi[:, x:x + 1], op0=ALU.max, op1=ALU.min)
+            nc.vector.tensor_scalar(out=q_phi[g][:, x, :], in0=q_aff[g][:, x, :], scalar1=qa_floor[:, x:x + 1],
+                                    scalar2=qa_sign[:, x:x + 1], op0=ALU.max, op1=ALU.mult)
 
         def q_views(half, s0, s1):
             g, u = divmod(half, 2)
@@ -253,15 +251,13 @@ def tile_rows_lin_relu1_norm_gate_kernel(tc, q, qa, ka, k, t, v, og, out):
                                 in1=t_sb[:].unsqueeze(1).unsqueeze(1).to_broadcast(shape), op=ALU.mult)
         dst, src = relu_views(0, *HEAD0_PIECES[0])
         nc.vector.tensor_scalar(out=dst, in0=src, scalar1=0.0, scalar2=None, op0=ALU.max)
-        nc.vector.tensor_scalar(out=qa8[:], in0=qa_sb[:], scalar1=PHI, scalar2=None, op0=ALU.mult)
-        nc.vector.tensor_scalar(out=qa_side[:], in0=qa_sb[:], scalar1=0.0, scalar2=0.5, op0=ALU.is_ge,
-                                op1=ALU.subtract)
         for piece in HEAD0_PIECES[1:]:
             relu_k(0, *piece)
+        nc.scalar.activation(out=qa_abs[:], in_=qa_sb[:], func=ACT.Abs)
+        nc.scalar.activation(out=qa_floor[:], in_=qa_sb[:], func=ACT.Abs, scale=PHI)
+        nc.scalar.activation(out=qa_sign[:], in_=qa_sb[:], func=ACT.Sign)
         for piece in HEAD0_PIECES:
             scale_k(0, *piece)
-        nc.vector.scalar_tensor_tensor(out=q_lo[:], in0=qa_side[:], scalar=BIG, in1=qa8[:], op0=ALU.mult, op1=ALU.min)
-        nc.vector.scalar_tensor_tensor(out=q_hi[:], in0=qa_side[:], scalar=BIG, in1=qa8[:], op0=ALU.mult, op1=ALU.max)
         quant_k(0)
         relu_k_halves(1)
         scale_k(1, 0)

@@ -58,9 +58,9 @@ def tile_rows_lin_relu1_norm_gate_kernel(tc, q, qa, ka, k, t, v, og, out):
         q_raw = tiles("q_raw", 4, [P, 2, N], F32)
         q_aff = tiles("q_aff", 2, [P, PACK, N], BF16)
         q_phi = tiles("q_phi", 2, [P, PACK, N], BF16)
+        qa_sign = tile("qa_sign", [P, PACK], F32)
         qa_abs = tile("qa_abs", [P, PACK], F32)
         qa_floor = tile("qa_floor", [P, PACK], F32)
-        qa_sign = tile("qa_sign", [P, PACK], F32)
         q_bf = tiles("q_bf", 4, [P, HALF, PACK], BF16)
         q_codes = tiles("q_codes", 4, [P, HALF], U32)
         q_scales = tiles("q_scales", 4, [P, HALF], U8)
@@ -249,13 +249,10 @@ def tile_rows_lin_relu1_norm_gate_kernel(tc, q, qa, ka, k, t, v, og, out):
         shape = [P, PACK, R, PACK]
         nc.vector.tensor_tensor(out=tka[:], in0=ka_sb[:].rearrange("p (m x) -> p x m", x=PACK).unsqueeze(3).to_broadcast(shape),
                                 in1=t_sb[:].unsqueeze(1).unsqueeze(1).to_broadcast(shape), op=ALU.mult)
-        dst, src = relu_views(0, *HEAD0_PIECES[0])
-        nc.vector.tensor_scalar(out=dst, in0=src, scalar1=0.0, scalar2=None, op0=ALU.max)
-        for piece in HEAD0_PIECES[1:]:
-            relu_k(0, *piece)
-        nc.scalar.activation(out=qa_abs[:], in_=qa_sb[:], func=ACT.Abs)
-        nc.scalar.activation(out=qa_floor[:], in_=qa_sb[:], func=ACT.Abs, scale=PHI)
-        nc.scalar.activation(out=qa_sign[:], in_=qa_sb[:], func=ACT.Sign)
+        for piece in HEAD0_PIECES[:2]:
+            dst, src = relu_views(0, *piece)
+            nc.vector.tensor_scalar(out=dst, in0=src, scalar1=0.0, scalar2=None, op0=ALU.max)
+        relu_k(0, 1)
         for piece in HEAD0_PIECES:
             scale_k(0, *piece)
         quant_k(0)
@@ -267,7 +264,11 @@ def tile_rows_lin_relu1_norm_gate_kernel(tc, q, qa, ka, k, t, v, og, out):
         cast_v_scalar(1)
         scale_k(2, 0)
         quant_k(1)
+        nc.vector.tensor_scalar(out=qa_sign[:], in0=qa_sb[:], scalar1=0.0, scalar2=0.5, op0=ALU.is_ge, op1=ALU.subtract)
         scale_k(2, 1)
+        nc.vector.scalar_tensor_tensor(out=qa_abs[:], in0=qa_sb[:], scalar=4.0, in1=qa_sign[:], op0=ALU.mult, op1=ALU.mult)
+        nc.vector.scalar_tensor_tensor(out=qa_floor[:], in0=qa_sb[:], scalar=4.0 * PHI, in1=qa_sign[:], op0=ALU.mult,
+                                       op1=ALU.mult)
         quant_v(0)
         mm_state(0)
         relu_k_halves(3)

@@ -135,7 +135,7 @@ def tile_rows_lin_relu1_norm_gate_kernel(tc, q, qa, ka, k, t, v, og, out):
                                       in_=src[:, n0 * D:n1 * D])
 
         def interleave_views(dst, src):
-            return dst.rearrange("p (b i) j -> p b j i", i=4), src.rearrange("p j (b i) -> p b j i", i=4)
+            return dst.rearrange("p (b i) j -> p b j i", i=2), src.rearrange("p j (b i) -> p b j i", i=2)
 
         def v_views(h):
             g, c = divmod(h, 2)
@@ -271,7 +271,10 @@ def tile_rows_lin_relu1_norm_gate_kernel(tc, q, qa, ka, k, t, v, og, out):
                                        op1=ALU.mult)
         quant_v(0)
         mm_state(0)
-        relu_k_halves(3)
+        relu_k(3, 0)
+        relu_k(3, 1, R // 2, R)
+        dst, src = relu_views(3, 1, 0, R // 2)
+        nc.vector.tensor_scalar(out=dst, in0=src, scalar1=0.0, scalar2=None, op0=ALU.max)
         scale_k(3, 0)
         scale_k(3, 1)
 

@@ -123,17 +123,6 @@ def tile_rows_lin_relu1_norm_gate_kernel(tc, q, qa, ka, k, t, v, og, out):
                 nc.vector.quantize_mx(out=k_codes[g][:, x, cols].bitcast(FP8X4), scales=k_scales[g][:, x, cols],
                                       in_=k_bf[g][:, x, c].rearrange("p m j -> p (m j)"))
 
-        def quant_k_pair(g):
-            src = k_bf[g][:].rearrange("p x c m j -> p (x c m j)")
-            codes = k_codes[g][:].rearrange("p x w -> p (x w)")
-            scales = k_scales[g][:].rearrange("p x w -> p (x w)")
-            for x in range(PACK + 1):
-                n0, n1 = max(2 * x - 1, 0), min(2 * x + 1, 2 * PACK)
-                w0 = max(3 * x - 1, 0) * R
-                cols = slice(w0, w0 + (n1 - n0) * R)
-                nc.vector.quantize_mx(out=codes[:, cols].bitcast(FP8X4), scales=scales[:, cols],
-                                      in_=src[:, n0 * D:n1 * D])
-
         def interleave_views(dst, src):
             return dst.rearrange("p (b i) j -> p b j i", i=2), src.rearrange("p j (b i) -> p b j i", i=2)
 
@@ -269,6 +258,7 @@ def tile_rows_lin_relu1_norm_gate_kernel(tc, q, qa, ka, k, t, v, og, out):
         nc.vector.scalar_tensor_tensor(out=qa_abs[:], in0=qa_sb[:], scalar=4.0, in1=qa_sign[:], op0=ALU.mult, op1=ALU.mult)
         nc.vector.scalar_tensor_tensor(out=qa_floor[:], in0=qa_sb[:], scalar=4.0 * PHI, in1=qa_sign[:], op0=ALU.mult,
                                        op1=ALU.mult)
+        quant_k(2)
         quant_v(0)
         mm_state(0)
         relu_k(3, 0)
@@ -281,7 +271,7 @@ def tile_rows_lin_relu1_norm_gate_kernel(tc, q, qa, ka, k, t, v, og, out):
         for x in range(3):
             affine_q_scalar(0, x)
         clamp_q(0, 0)
-        quant_k_pair(1)
+        quant_k(3)
         affine_q_vector(0, 3)
         for x in range(1, PACK):
             clamp_q(0, x)

@@ -21,7 +21,8 @@ HALF = N // 2
 PHI = 0.125
 HEAD0_PIECES = ((0, 0, 32), (0, 32, R), (1, 0, R))
 VECTOR_COLUMNS_HALF0 = 80
-VECTOR_COLUMNS_HALF3 = 64
+HALF1_CUT = 96
+VECTOR_COLUMNS_HALF3 = 40
 
 
 def tile_rows_lin_relu1_norm_gate_kernel(tc, q, qa, ka, k, t, v, og, out):
@@ -216,6 +217,9 @@ def tile_rows_lin_relu1_norm_gate_kernel(tc, q, qa, ka, k, t, v, og, out):
                                                scalar=rden[bank][:, slot + r:slot + r + 1],
                                                in1=gate[g][:, c, u, r, :], op0=ALU.mult, op1=ALU.mult)
 
+        def sigmoid(g, c, us):
+            nc.scalar.activation(out=gate[g][:, c, us], in_=og_raw[g][:, c, us], func=ACT.Sigmoid)
+
         nc.scalar.dma_start(out=t_sb[:], in_=t.rearrange("(p j) o -> p (j o)", j=PACK))
         for c in range(2):
             nc.scalar.dma_start(out=qa_sb[R * c:R * c + R, :], in_=qa.rearrange("(m x) o -> m (x o)", x=PACK))
@@ -244,7 +248,11 @@ def tile_rows_lin_relu1_norm_gate_kernel(tc, q, qa, ka, k, t, v, og, out):
         relu_k(0, 1)
         for piece in HEAD0_PIECES:
             scale_k(0, *piece)
+        nc.vector.tensor_scalar(out=qa_sign[:], in0=qa_sb[:], scalar1=0.0, scalar2=0.5, op0=ALU.is_ge, op1=ALU.subtract)
         quant_k(0)
+        nc.vector.scalar_tensor_tensor(out=qa_abs[:], in0=qa_sb[:], scalar=4.0, in1=qa_sign[:], op0=ALU.mult, op1=ALU.mult)
+        nc.vector.scalar_tensor_tensor(out=qa_floor[:], in0=qa_sb[:], scalar=4.0 * PHI, in1=qa_sign[:], op0=ALU.mult,
+                                       op1=ALU.mult)
         relu_k_halves(1)
         scale_k(1, 0)
         scale_k(1, 1)
@@ -253,11 +261,7 @@ def tile_rows_lin_relu1_norm_gate_kernel(tc, q, qa, ka, k, t, v, og, out):
         cast_v_scalar(1)
         scale_k(2, 0)
         quant_k(1)
-        nc.vector.tensor_scalar(out=qa_sign[:], in0=qa_sb[:], scalar1=0.0, scalar2=0.5, op0=ALU.is_ge, op1=ALU.subtract)
         scale_k(2, 1)
-        nc.vector.scalar_tensor_tensor(out=qa_abs[:], in0=qa_sb[:], scalar=4.0, in1=qa_sign[:], op0=ALU.mult, op1=ALU.mult)
-        nc.vector.scalar_tensor_tensor(out=qa_floor[:], in0=qa_sb[:], scalar=4.0 * PHI, in1=qa_sign[:], op0=ALU.mult,
-                                       op1=ALU.mult)
         quant_k(2)
         quant_v(0)
         mm_state(0)
@@ -271,56 +275,62 @@ def tile_rows_lin_relu1_norm_gate_kernel(tc, q, qa, ka, k, t, v, og, out):
         for x in range(3):
             affine_q_scalar(0, x)
         clamp_q(0, 0)
-        quant_k(3)
         affine_q_vector(0, 3)
-        for x in range(1, PACK):
+        quant_k(3)
+        for x in (3, 1, 2):
             clamp_q(0, x)
         read_state(0)
         cast_v_scalar(2)
         cast_v_vector(3)
-        quant_s(0)
         interleave_q_scalar(0, VECTOR_COLUMNS_HALF0, P)
         interleave_q_vector(0, 0, VECTOR_COLUMNS_HALF0)
+        quant_s(0)
         quant_v(1)
         mm_state(1)
-        interleave_q_vector(1, 0, P)
+        interleave_q_vector(1, 0, HALF1_CUT)
         quant_q(0)
         mm_read(0)
 
         for x in range(3):
             affine_q_scalar(1, x)
+        clamp_q(1, 0)
         affine_q_vector(1, 3)
-        for x in (0, 1, 3, 2):
-            clamp_q(1, x)
+        clamp_q(1, 1)
+        interleave_q_vector(1, HALF1_CUT, P)
+        clamp_q(1, 3)
+        clamp_q(1, 2)
         quant_q(1)
         mm_read(1)
         read_state(1)
         interleave_q_scalar(3, VECTOR_COLUMNS_HALF3, P)
-        for c in (1, 0):
-            nc.scalar.activation(out=gate[0][:, c], in_=og_raw[0][:, c], func=ACT.Sigmoid)
+        sigmoid(0, 1, slice(0, 2))
+        sigmoid(0, 0, 0)
         interleave_q_vector(2, 0, P)
-        quant_s(1)
         interleave_q_vector(3, 0, VECTOR_COLUMNS_HALF3)
-        recip(0, 4)
+        quant_s(1)
+        quant_q(2)
+        mm_read(2)
         recip(1, 4)
-        for half in (2, 3):
-            quant_q(half)
-            mm_read(half)
+        recip(0, 4)
+        quant_q(3)
+        mm_read(3)
 
         finish(0, 1)
         store(0, 1, nc.sync)
         for r in range(2):
             nc.scalar.activation(out=y_norm[:, r, :], in_=y_ps[0][:, r, :], func=ACT.Copy, scale=rden[0][:, r:r + 1])
         nc.gpsimd.tensor_tensor(out=res[0][:, 0, 0], in0=y_norm[:], in1=gate[0][:, 0, 0], op=ALU.mult)
-        for u in range(2):
-            nc.scalar.activation(out=gate[1][:, :, u], in_=og_raw[1][:, :, u], func=ACT.Sigmoid)
+        sigmoid(0, 0, 1)
+        sigmoid(1, 0, 0)
+        sigmoid(1, 1, 0)
+        sigmoid(1, 0, 1)
+        sigmoid(1, 1, 1)
         store(0, 0, nc.scalar)
         finish(1, 1)
         store(1, 1, nc.sync)
-        finish(1, 0, (0,))
         recip(2, 2)
         recip(3, 2)
-        finish(1, 0, (1,))
+        finish(1, 0)
         store(1, 0, nc.sync)
         finish(2, 0)
         store(2, 0, nc.scalar)

@@ -93,12 +93,24 @@ def tile_rows_lin_relu1_norm_gate_kernel(tc, q, qa, ka, k, t, v, og, out):
         def row_pairs(x, g):
             return x[2 * g:2 * g + 2].rearrange("c (u s r) e -> s (c u) (r e)", u=2, r=2)
 
-        def load_og(g):
-            nc.sync.dma_start(out=og_raw[g][:].rearrange("p c u r e -> p (c u) (r e)"), in_=row_pairs(og, g))
+        def load_og(g, c0=0, c1=2):
+            nc.sync.dma_start(out=og_raw[g][:, c0:c1].rearrange("p c u r e -> p (c u) (r e)"),
+                              in_=row_pairs(og, g)[:, 2 * c0:2 * c1, :])
 
         def store(half, c, queue):
             g, u = divmod(half, 2)
             queue.dma_start(out=row_pairs(out, g)[:, 2 * c + u, :], in_=res[g][:, c, u].rearrange("p r e -> p (r e)"))
+
+        def store_head(g, c, queue):
+            queue.dma_start(out=row_pairs(out, g)[:, 2 * c:2 * c + 2, :], in_=res[g][:, c].rearrange("p u r e -> p u (r e)"))
+
+        def store_half(half, queue):
+            g, u = divmod(half, 2)
+            queue.dma_start(out=row_pairs(out, g)[:, u::2, :], in_=res[g][:, :, u].rearrange("p c r e -> p c (r e)"))
+
+        def store_row(half, c, r, queue):
+            g, u = divmod(half, 2)
+            queue.dma_start(out=row_pairs(out, g)[:, 2 * c + u, E * r:E * r + E], in_=res[g][:, c, u, r])
 
         def relu_views(h, y, m0, m1):
             return (k_relu[h][:, 2 * y:2 * y + 2, m0:m1, :].rearrange("p x m j -> p m j x"),
@@ -220,17 +232,56 @@ def tile_rows_lin_relu1_norm_gate_kernel(tc, q, qa, ka, k, t, v, og, out):
         def sigmoid(g, c, us):
             nc.scalar.activation(out=gate[g][:, c, us], in_=og_raw[g][:, c, us], func=ACT.Sigmoid)
 
-        nc.scalar.dma_start(out=t_sb[:], in_=t.rearrange("(p j) o -> p (j o)", j=PACK))
-        for c in range(2):
-            nc.scalar.dma_start(out=qa_sb[R * c:R * c + R, :], in_=qa.rearrange("(m x) o -> m (x o)", x=PACK))
-        nc.vector.memset(table_in[:], 0.0)
-        nc.scalar.activation(out=table_out[:], in_=table_in[:], func=ACT.Sigmoid)
-        for g in range(2):
-            nc.gpsimd.memset(k_codes[g][:, :, R:2 * R], 0)
-            nc.gpsimd.memset(k_scales[g][:].bitcast(I32)[:, :, R // 4:R // 2], 0)
+        def small_loads():
+            nc.scalar.dma_start(out=t_sb[:], in_=t.rearrange("(p j) o -> p (j o)", j=PACK))
+            for c in range(2):
+                nc.scalar.dma_start(out=qa_sb[R * c:R * c + R, :], in_=qa.rearrange("(m x) o -> m (x o)", x=PACK))
+
+        def zero_columns():
+            for g in range(2):
+                nc.gpsimd.memset(k_codes[g][:, :, R:2 * R], 0)
+                nc.gpsimd.memset(k_scales[g][:].bitcast(I32)[:, :, R // 4:R // 2], 0)
+
+        def load_q_places(g, i):
+            src = q[2 * g:2 * g + 2].rearrange("c (m x) n -> (c m) x n", x=PACK)
+            nc.sync.dma_start(out=q_raw[2 * g + i][:], in_=src[:, 2 * i:2 * i + 2, :])
+
+        def make_tka():
+            shape = [P, PACK, R, PACK]
+            nc.vector.tensor_tensor(out=tka[:], in0=ka_sb[:].rearrange("p (m x) -> p x m", x=PACK).unsqueeze(3).to_broadcast(shape),
+                                    in1=t_sb[:].unsqueeze(1).unsqueeze(1).to_broadcast(shape), op=ALU.mult)
+
+        def relu_k_vector(h, y, m0=0, m1=R):
+            dst, src = relu_views(h, y, m0, m1)
+            nc.vector.tensor_scalar(out=dst, in0=src, scalar1=0.0, scalar2=None, op0=ALU.max)
+
+        def make_sign():
+            nc.vector.tensor_scalar(out=qa_sign[:], in0=qa_sb[:], scalar1=0.0, scalar2=0.5, op0=ALU.is_ge, op1=ALU.subtract)
+
+        def make_abs_floor():
+            nc.vector.scalar_tensor_tensor(out=qa_abs[:], in0=qa_sb[:], scalar=4.0, in1=qa_sign[:], op0=ALU.mult, op1=ALU.mult)
+            nc.vector.scalar_tensor_tensor(out=qa_floor[:], in0=qa_sb[:], scalar=4.0 * PHI, in1=qa_sign[:], op0=ALU.mult,
+                                           op1=ALU.mult)
+
+        def affine_q_gpsimd(g, x):
+            dst, src = affine_views(g, x)
+            nc.gpsimd.tensor_scalar(out=dst, in0=src, scalar1=qa_abs[:, x:x + 1], scalar2=qa_floor[:, x:x + 1],
+                                    op0=ALU.mult, op1=ALU.add)
+
+        def norm_scalar(half, c):
+            bank, slot = y_place(half, c)
+            for r in range(2):
+                nc.scalar.activation(out=y_norm[:, r, :], in_=y_ps[bank][:, slot + r, :], func=ACT.Copy,
+                                     scale=rden[bank][:, slot + r:slot + r + 1])
+
+        def gate_gpsimd(half, c):
+            g, u = divmod(half, 2)
+            nc.gpsimd.tensor_tensor(out=res[g][:, c, u], in0=y_norm[:], in1=gate[g][:, c, u], op=ALU.mult)
+
         nc.sync.dma_start(out=ka_sb[:], in_=ka)
-        for h in range(3):
-            load_k(h)
+        load_k(0)
+        load_k(1)
+        load_k(2)
         load_v(0)
         load_k(3)
         load_q(0)
@@ -238,94 +289,91 @@ def tile_rows_lin_relu1_norm_gate_kernel(tc, q, qa, ka, k, t, v, og, out):
         load_q(1)
         load_og(0)
         load_og(1)
-
-        shape = [P, PACK, R, PACK]
-        nc.vector.tensor_tensor(out=tka[:], in0=ka_sb[:].rearrange("p (m x) -> p x m", x=PACK).unsqueeze(3).to_broadcast(shape),
-                                in1=t_sb[:].unsqueeze(1).unsqueeze(1).to_broadcast(shape), op=ALU.mult)
-        for piece in HEAD0_PIECES[:2]:
-            dst, src = relu_views(0, *piece)
-            nc.vector.tensor_scalar(out=dst, in0=src, scalar1=0.0, scalar2=None, op0=ALU.max)
+        zero_columns()
+        small_loads()
+        nc.vector.memset(table_in[:], 0.0)
+        nc.scalar.activation(out=table_out[:], in_=table_in[:], func=ACT.Sigmoid)
         relu_k(0, 1)
-        for piece in HEAD0_PIECES:
-            scale_k(0, *piece)
-        nc.vector.tensor_scalar(out=qa_sign[:], in0=qa_sb[:], scalar1=0.0, scalar2=0.5, op0=ALU.is_ge, op1=ALU.subtract)
-        quant_k(0)
-        nc.vector.scalar_tensor_tensor(out=qa_abs[:], in0=qa_sb[:], scalar=4.0, in1=qa_sign[:], op0=ALU.mult, op1=ALU.mult)
-        nc.vector.scalar_tensor_tensor(out=qa_floor[:], in0=qa_sb[:], scalar=4.0 * PHI, in1=qa_sign[:], op0=ALU.mult,
-                                       op1=ALU.mult)
         relu_k_halves(1)
-        scale_k(1, 0)
-        scale_k(1, 1)
         relu_k_halves(2)
         cast_v_scalar(0)
         cast_v_scalar(1)
+        relu_k(3, 0)
+        relu_k(3, 1, 32, R)
+        make_tka()
+        relu_k_vector(0, 0, 0, 32)
+        relu_k_vector(0, 0, 32, R)
+        scale_k(0, 0, 0, 32)
+        scale_k(0, 0, 32, R)
+        scale_k(0, 1)
+        make_sign()
+        quant_k(0)
+        make_abs_floor()
+        affine_q_scalar(0, 0)
+        affine_q_scalar(0, 1)
+        affine_q_scalar(0, 2)
+        scale_k(1, 0)
+        scale_k(1, 1)
         scale_k(2, 0)
         quant_k(1)
         scale_k(2, 1)
         quant_k(2)
         quant_v(0)
         mm_state(0)
-        relu_k(3, 0)
-        relu_k(3, 1, R // 2, R)
-        dst, src = relu_views(3, 1, 0, R // 2)
-        nc.vector.tensor_scalar(out=dst, in0=src, scalar1=0.0, scalar2=None, op0=ALU.max)
+        read_state(0)
+        cast_v_scalar(2)
+        relu_k_vector(3, 1, 0, 32)
         scale_k(3, 0)
         scale_k(3, 1)
-
-        for x in range(3):
-            affine_q_scalar(0, x)
         clamp_q(0, 0)
         affine_q_vector(0, 3)
         quant_k(3)
-        for x in (3, 1, 2):
-            clamp_q(0, x)
-        read_state(0)
-        cast_v_scalar(2)
+        clamp_q(0, 3)
+        clamp_q(0, 1)
+        clamp_q(0, 2)
+        interleave_q_scalar(0, 80, P)
+        affine_q_scalar(1, 0)
+        affine_q_scalar(1, 1)
+        affine_q_scalar(1, 2)
         cast_v_vector(3)
-        interleave_q_scalar(0, VECTOR_COLUMNS_HALF0, P)
-        interleave_q_vector(0, 0, VECTOR_COLUMNS_HALF0)
+        interleave_q_vector(0, 0, 80)
         quant_s(0)
         quant_v(1)
         mm_state(1)
-        interleave_q_vector(1, 0, HALF1_CUT)
+        read_state(1)
+        interleave_q_vector(1, 0, 96)
         quant_q(0)
         mm_read(0)
-
-        for x in range(3):
-            affine_q_scalar(1, x)
         clamp_q(1, 0)
         affine_q_vector(1, 3)
         clamp_q(1, 1)
-        interleave_q_vector(1, HALF1_CUT, P)
+        interleave_q_vector(1, 96, P)
         clamp_q(1, 3)
         clamp_q(1, 2)
-        quant_q(1)
-        mm_read(1)
-        read_state(1)
-        interleave_q_scalar(3, VECTOR_COLUMNS_HALF3, P)
+        interleave_q_scalar(3, 40, P)
         sigmoid(0, 1, slice(0, 2))
         sigmoid(0, 0, 0)
+        quant_q(1)
+        mm_read(1)
         interleave_q_vector(2, 0, P)
-        interleave_q_vector(3, 0, VECTOR_COLUMNS_HALF3)
+        interleave_q_vector(3, 0, 40)
         quant_s(1)
         quant_q(2)
         mm_read(2)
         recip(1, 4)
         recip(0, 4)
-        quant_q(3)
-        mm_read(3)
-
-        finish(0, 1)
-        store(0, 1, nc.sync)
-        for r in range(2):
-            nc.scalar.activation(out=y_norm[:, r, :], in_=y_ps[0][:, r, :], func=ACT.Copy, scale=rden[0][:, r:r + 1])
-        nc.gpsimd.tensor_tensor(out=res[0][:, 0, 0], in0=y_norm[:], in1=gate[0][:, 0, 0], op=ALU.mult)
+        norm_scalar(0, 0)
+        gate_gpsimd(0, 0)
         sigmoid(0, 0, 1)
         sigmoid(1, 0, 0)
         sigmoid(1, 1, 0)
         sigmoid(1, 0, 1)
         sigmoid(1, 1, 1)
         store(0, 0, nc.scalar)
+        quant_q(3)
+        mm_read(3)
+        finish(0, 1)
+        store(0, 1, nc.sync)
         finish(1, 1)
         store(1, 1, nc.sync)
         recip(2, 2)
@@ -333,12 +381,12 @@ def tile_rows_lin_relu1_norm_gate_kernel(tc, q, qa, ka, k, t, v, og, out):
         finish(1, 0)
         store(1, 0, nc.sync)
         finish(2, 0)
-        store(2, 0, nc.scalar)
+        store(2, 0, nc.sync)
         recip(4, 2)
         recip(5, 2)
         finish(2, 1)
         store(2, 1, nc.sync)
         finish(3, 0)
-        store(3, 0, nc.scalar)
+        store(3, 0, nc.sync)
         finish(3, 1)
         store(3, 1, nc.sync)

@@ -164,6 +164,22 @@ def tile_rows_lin_relu1_norm_gate_kernel(tc, q, qa, ka, k, t, v, og, out):
                                         lhsT_scale=k_scales[g][:, x, cols], rhs=v_codes[g][:, vc].bitcast(FP8X4),
                                         rhs_scale=v_scales[g][:, vc], start=(c == 0), stop=(c == 1))
 
+        def quant_v_head(h):
+            g, c = divmod(h, 2)
+            vc = slice(E * c, E * c + E)
+            nc.vector.quantize_mx(out=v_codes[g][:, vc].bitcast(FP8X4), scales=v_scales[g][:, vc],
+                                  in_=v_bf[g][:, c].rearrange("p e j -> p (e j)"))
+
+        def mm_state_head(h, first):
+            g, c = divmod(h, 2)
+            cols = slice(R * c, R * c + P)
+            vc = slice(E * c, E * c + E)
+            for x in range(PACK):
+                nc.tensor.matmul_mx(out=s_ps[g][:, x, :], lhsT=k_codes[g][:, x, cols].bitcast(FP8X4),
+                                    lhsT_scale=k_scales[g][:, x, cols], rhs=v_codes[g][:, vc].bitcast(FP8X4),
+                                    rhs_scale=v_scales[g][:, vc], start=(first and x == 0),
+                                    stop=(not first and x == PACK - 1))
+
         def read_state(g):
             nc.scalar.activation(out=s_bf[g][:], in_=s_ps[g][:].rearrange("p x e -> p e x"), func=ACT.Copy,
                                  scale=1.0 / N)
@@ -337,9 +353,11 @@ def tile_rows_lin_relu1_norm_gate_kernel(tc, q, qa, ka, k, t, v, og, out):
         affine_q_scalar(1, 2)
         cast_v_vector(3)
         interleave_q_vector(0, 0, 80)
+        quant_v_head(3)
+        mm_state_head(3, True)
         quant_s(0)
-        quant_v(1)
-        mm_state(1)
+        quant_v_head(2)
+        mm_state_head(2, False)
         read_state(1)
         interleave_q_vector(1, 0, 96)
         quant_q(0)

@@ -33,7 +33,7 @@ def tile_rows_lin_relu1_norm_gate_kernel(tc, q, qa, ka, k, t, v, og, out):
         ctx.enter_context(tc.manual_schedule())
 
         def tile(name, shape, dtype):
-            return sb.tile(shape, dtype, name=name, align_bytes=64)
+            return sb.tile(shape, dtype, name=name, align_bytes=256)
 
         def tiles(name, count, shape, dtype):
             return [tile("%s_%d" % (name, i), shape, dtype) for i in range(count)]

from contextlib import ExitStack

import concourse.mybir as mybir

H, D, N, E = 4, 256, 512, 128
FLOPS = 2 * 2 * H * D * N * E

F32 = mybir.dt.float32
BF16 = mybir.dt.bfloat16
U32 = mybir.dt.uint32
I32 = mybir.dt.int32
U8 = mybir.dt.uint8
FP8X4 = mybir.dt.float8_e4m3fn_x4
ACT = mybir.ActivationFunctionType
ALU = mybir.AluOpType

P = 128
R = 64
PACK = 4
HALF = N // 2
PHI = 0.125
HEAD0_PIECES = ((0, 0, 32), (0, 32, R), (1, 0, R))
VECTOR_COLUMNS_HALF0 = 80
HALF1_CUT = 96
VECTOR_COLUMNS_HALF3 = 40


def tile_rows_lin_relu1_norm_gate_kernel(tc, q, qa, ka, k, t, v, og, out):
    nc = tc.nc
    with ExitStack() as ctx:
        sb = ctx.enter_context(tc.tile_pool(name="sb", bufs=1))
        ps = ctx.enter_context(tc.psum_pool(name="ps", bufs=1))
        ctx.enter_context(tc.manual_schedule())

        def tile(name, shape, dtype):
            return sb.tile(shape, dtype, name=name, align_bytes=256)

        def tiles(name, count, shape, dtype):
            return [tile("%s_%d" % (name, i), shape, dtype) for i in range(count)]

        t_sb = tile("t_sb", [P, PACK], F32)
        qa_sb = tile("qa_sb", [P, PACK], F32)
        ka_sb = tile("ka_sb", [P, D], F32)
        tka = tile("tka", [P, PACK, R, PACK], F32)
        table_in = tile("table_in", [P, 8], F32)
        table_out = tile("table_out", [P, 8], F32)
        k_raw = tiles("k_raw", H, [P, PACK, D], F32)
        k_relu = tiles("k_relu", H, [P, PACK, R, PACK], F32)
        k_bf = tiles("k_bf", 2, [P, PACK, 2, R, PACK], BF16)
        k_codes = tiles("k_codes", 2, [P, PACK, 3 * R], U32)
        k_scales = tiles("k_scales", 2, [P, PACK, 3 * R], U8)
        v_raw = tiles("v_raw", 2, [P, 2, PACK, E], F32)
        v_bf = tiles("v_bf", 2, [P, 2, E, PACK], BF16)
        v_codes = tiles("v_codes", 2, [P, 2 * E], U32)
        v_scales = tiles("v_scales", 2, [P, 2 * E], U8)
        s_bf = tiles("s_bf", 2, [P, E, PACK], BF16)
        s_codes = tiles("s_codes", 2, [P, E], U32)
        s_scales = tiles("s_scales", 2, [P, E], U8)
        q_raw = tiles("q_raw", 4, [P, 2, N], F32)
        q_aff = tiles("q_aff", 2, [P, PACK, N], BF16)
        q_phi = tiles("q_phi", 2, [P, PACK, N], BF16)
        qa_sign = tile("qa_sign", [P, PACK], F32)
        qa_abs = tile("qa_abs", [P, PACK], F32)
        qa_floor = tile("qa_floor", [P, PACK], F32)
        q_bf = tiles("q_bf", 4, [P, HALF, PACK], BF16)
        q_codes = tiles("q_codes", 4, [P, HALF], U32)
        q_scales = tiles("q_scales", 4, [P, HALF], U8)
        og_raw = tiles("og_raw", 2, [P, 2, 2, 2, E], F32)
        gate = tiles("gate", 2, [P, 2, 2, 2, E], F32)
        res = tiles("res", 2, [P, 2, 2, 2, E], F32)
        y_norm = tile("y_norm", [P, 2, E], F32)
        rden = tiles("rden", 6, [P, 4], F32)
        s_ps = [ps.tile([P, PACK, E], F32, name="s_ps_%d" % g) for g in range(2)]
        y_ps = [ps.tile([P, 4, E], F32, name="y_ps_%d" % b) for b in range(6)]

        def y_place(half, c):
            if half < 2:
                return c, 2 * half
            return 2 * (half - 1) + c, 0

        def load_k(h):
            nc.sync.dma_start(out=k_raw[h][:], in_=k[h].rearrange("(p j) d -> p j d", j=PACK))

        def load_v(g):
            nc.sync.dma_start(out=v_raw[g][:].rearrange("p c j e -> p c (j e)"),
                              in_=v[2 * g:2 * g + 2].rearrange("c (p j) e -> p c (j e)", j=PACK))

        def load_q(g):
            src = q[2 * g:2 * g + 2].rearrange("c (m x) n -> (c m) x n", x=PACK)
            for i in range(2):
                nc.sync.dma_start(out=q_raw[2 * g + i][:], in_=src[:, 2 * i:2 * i + 2, :])

        def row_pairs(x, g):
            return x[2 * g:2 * g + 2].rearrange("c (u s r) e -> s (c u) (r e)", u=2, r=2)

        def load_og(g, c0=0, c1=2):
            nc.sync.dma_start(out=og_raw[g][:, c0:c1].rearrange("p c u r e -> p (c u) (r e)"),
                              in_=row_pairs(og, g)[:, 2 * c0:2 * c1, :])

        def store(half, c, queue):
            g, u = divmod(half, 2)
            queue.dma_start(out=row_pairs(out, g)[:, 2 * c + u, :], in_=res[g][:, c, u].rearrange("p r e -> p (r e)"))

        def store_head(g, c, queue):
            queue.dma_start(out=row_pairs(out, g)[:, 2 * c:2 * c + 2, :], in_=res[g][:, c].rearrange("p u r e -> p u (r e)"))

        def store_half(half, queue):
            g, u = divmod(half, 2)
            queue.dma_start(out=row_pairs(out, g)[:, u::2, :], in_=res[g][:, :, u].rearrange("p c r e -> p c (r e)"))

        def store_row(half, c, r, queue):
            g, u = divmod(half, 2)
            queue.dma_start(out=row_pairs(out, g)[:, 2 * c + u, E * r:E * r + E], in_=res[g][:, c, u, r])

        def relu_views(h, y, m0, m1):
            return (k_relu[h][:, 2 * y:2 * y + 2, m0:m1, :].rearrange("p x m j -> p m j x"),
                    k_raw[h][:].rearrange("p j (m x) -> p m j x", x=PACK)[:, m0:m1, :, 2 * y:2 * y + 2])

        def relu_k(h, y, m0=0, m1=R):
            dst, src = relu_views(h, y, m0, m1)
            nc.scalar.activation(out=dst, in_=src, func=ACT.Relu)

        def relu_k_halves(h):
            relu_k(h, 0)
            relu_k(h, 1)

        def scale_k(h, y, m0=0, m1=R):
            xs = slice(2 * y, 2 * y + 2)
            nc.vector.scalar_tensor_tensor(out=k_bf[h // 2][:, xs, h % 2, m0:m1, :], in0=k_relu[h][:, xs, m0:m1, :], scalar=PHI,
                                           in1=tka[:, xs, m0:m1, :], op0=ALU.add, op1=ALU.mult)

        def quant_k(h):
            g, c = divmod(h, 2)
            cols = slice(2 * R * c, 2 * R * c + R)
            for x in range(PACK):
                nc.vector.quantize_mx(out=k_codes[g][:, x, cols].bitcast(FP8X4), scales=k_scales[g][:, x, cols],
                                      in_=k_bf[g][:, x, c].rearrange("p m j -> p (m j)"))

        def interleave_views(dst, src):
            return dst.rearrange("p (b i) j -> p b j i", i=2), src.rearrange("p j (b i) -> p b j i", i=2)

        def v_views(h):
            g, c = divmod(h, 2)
            return interleave_views(v_bf[g][:, c], v_raw[g][:, c])

        def cast_v_scalar(h):
            dst, src = v_views(h)
            nc.scalar.copy(out=dst, in_=src)

        def cast_v_vector(h):
            dst, src = v_views(h)
            nc.vector.tensor_copy(out=dst, in_=src)

        def quant_v(g):
            nc.vector.quantize_mx(out=v_codes[g][:].bitcast(FP8X4), scales=v_scales[g][:],
                                  in_=v_bf[g][:].rearrange("p c e j -> p (c e j)"))

        def mm_state(g):
            for x in range(PACK):
                for c in range(2):
                    cols = slice(R * c, R * c + P)
                    vc = slice(E * c, E * c + E)
                    nc.tensor.matmul_mx(out=s_ps[g][:, x, :], lhsT=k_codes[g][:, x, cols].bitcast(FP8X4),
                                        lhsT_scale=k_scales[g][:, x, cols], rhs=v_codes[g][:, vc].bitcast(FP8X4),
                                        rhs_scale=v_scales[g][:, vc], start=(c == 0), stop=(c == 1))

        def quant_v_head(h):
            g, c = divmod(h, 2)
            vc = slice(E * c, E * c + E)
            nc.vector.quantize_mx(out=v_codes[g][:, vc].bitcast(FP8X4), scales=v_scales[g][:, vc],
                                  in_=v_bf[g][:, c].rearrange("p e j -> p (e j)"))

        def mm_state_head(h, first):
            g, c = divmod(h, 2)
            cols = slice(R * c, R * c + P)
            vc = slice(E * c, E * c + E)
            for x in range(PACK):
                nc.tensor.matmul_mx(out=s_ps[g][:, x, :], lhsT=k_codes[g][:, x, cols].bitcast(FP8X4),
                                    lhsT_scale=k_scales[g][:, x, cols], rhs=v_codes[g][:, vc].bitcast(FP8X4),
                                    rhs_scale=v_scales[g][:, vc], start=(first and x == 0),
                                    stop=(not first and x == PACK - 1))

        def read_state(g):
            nc.scalar.activation(out=s_bf[g][:], in_=s_ps[g][:].rearrange("p x e -> p e x"), func=ACT.Copy,
                                 scale=1.0 / N)

        def quant_s(g):
            nc.vector.quantize_mx(out=s_codes[g][:].bitcast(FP8X4), scales=s_scales[g][:],
                                  in_=s_bf[g][:].rearrange("p e x -> p (e x)"))

        def affine_views(g, x):
            return q_aff[g][:, x, :], q_raw[2 * g + x // 2][:, x % 2, :]

        def affine_q_scalar(g, x):
            dst, src = affine_views(g, x)
            nc.scalar.activation(out=dst, in_=src, func=ACT.Identity, scale=qa_abs[:, x:x + 1], bias=qa_floor[:, x:x + 1])

        def affine_q_vector(g, x):
            dst, src = affine_views(g, x)
            nc.vector.tensor_scalar(out=dst, in0=src, scalar1=qa_abs[:, x:x + 1], scalar2=qa_floor[:, x:x + 1],
                                    op0=ALU.mult, op1=ALU.add)

        def clamp_q(g, x):
            nc.vector.tensor_scalar(out=q_phi[g][:, x, :], in0=q_aff[g][:, x, :], scalar1=qa_floor[:, x:x + 1],
                                    scalar2=qa_sign[:, x:x + 1], op0=ALU.max, op1=ALU.mult)

        def q_views(half, s0, s1):
            g, u = divmod(half, 2)
            dst = q_bf[half][:].rearrange("p (r s) x -> p s r x", r=2)[:, s0:s1]
            src = q_phi[g][:, :, HALF * u + 2 * s0:HALF * u + 2 * s1]
            return dst.rearrange("p (b i) r x -> p b x i r", i=2), src.rearrange("p x (b i r) -> p b x i r", i=2, r=2)

        def interleave_q_vector(half, n0, n1):
            dst, src = q_views(half, n0, n1)
            nc.vector.tensor_copy(out=dst, in_=src)

        def interleave_q_scalar(half, n0, n1):
            dst, src = q_views(half, n0, n1)
            nc.scalar.copy(out=dst, in_=src)

        def quant_q(half):
            nc.vector.quantize_mx(out=q_codes[half][:].bitcast(FP8X4), scales=q_scales[half][:],
                                  in_=q_bf[half][:].rearrange("p n x -> p (n x)"))

        def mm_read(half):
            g = half // 2
            for r in range(2):
                cols = slice(P * r, P * r + P)
                for c in range(2):
                    bank, slot = y_place(half, c)
                    part = slice(R * c, R * c + R)
                    nc.tensor.matmul_mx(out=y_ps[bank][:, slot + r, :],
                                        lhsT=q_codes[half][part, cols].bitcast(FP8X4),
                                        lhsT_scale=q_scales[half][part, cols], rhs=s_codes[g][part, :].bitcast(FP8X4),
                                        rhs_scale=s_scales[g][part, :], start=True, stop=True)

        def recip(bank, slots):
            nc.vector.reciprocal(out=rden[bank][:, 0:slots], in_=y_ps[bank][:, 0:slots, E - 1])

        def finish(half, c, rows=(0, 1)):
            g, u = divmod(half, 2)
            bank, slot = y_place(half, c)
            for r in rows:
                nc.vector.scalar_tensor_tensor(out=res[g][:, c, u, r, :], in0=y_ps[bank][:, slot + r, :],
                                               scalar=rden[bank][:, slot + r:slot + r + 1],
                                               in1=gate[g][:, c, u, r, :], op0=ALU.mult, op1=ALU.mult)

        def sigmoid(g, c, us):
            nc.scalar.activation(out=gate[g][:, c, us], in_=og_raw[g][:, c, us], func=ACT.Sigmoid)

        def small_loads():
            nc.scalar.dma_start(out=t_sb[:], in_=t.rearrange("(p j) o -> p (j o)", j=PACK))
            for c in range(2):
                nc.scalar.dma_start(out=qa_sb[R * c:R * c + R, :], in_=qa.rearrange("(m x) o -> m (x o)", x=PACK))

        def zero_columns():
            for g in range(2):
                nc.gpsimd.memset(k_codes[g][:, :, R:2 * R], 0)
                nc.gpsimd.memset(k_scales[g][:].bitcast(I32)[:, :, R // 4:R // 2], 0)

        def load_q_places(g, i):
            src = q[2 * g:2 * g + 2].rearrange("c (m x) n -> (c m) x n", x=PACK)
            nc.sync.dma_start(out=q_raw[2 * g + i][:], in_=src[:, 2 * i:2 * i + 2, :])

        def make_tka():
            shape = [P, PACK, R, PACK]
            nc.vector.tensor_tensor(out=tka[:], in0=ka_sb[:].rearrange("p (m x) -> p x m", x=PACK).unsqueeze(3).to_broadcast(shape),
                                    in1=t_sb[:].unsqueeze(1).unsqueeze(1).to_broadcast(shape), op=ALU.mult)

        def relu_k_vector(h, y, m0=0, m1=R):
            dst, src = relu_views(h, y, m0, m1)
            nc.vector.tensor_scalar(out=dst, in0=src, scalar1=0.0, scalar2=None, op0=ALU.max)

        def make_sign():
            nc.vector.tensor_scalar(out=qa_sign[:], in0=qa_sb[:], scalar1=0.0, scalar2=0.5, op0=ALU.is_ge, op1=ALU.subtract)

        def make_abs_floor():
            nc.vector.scalar_tensor_tensor(out=qa_abs[:], in0=qa_sb[:], scalar=4.0, in1=qa_sign[:], op0=ALU.mult, op1=ALU.mult)
            nc.vector.scalar_tensor_tensor(out=qa_floor[:], in0=qa_sb[:], scalar=4.0 * PHI, in1=qa_sign[:], op0=ALU.mult,
                                           op1=ALU.mult)

        def affine_q_gpsimd(g, x):
            dst, src = affine_views(g, x)
            nc.gpsimd.tensor_scalar(out=dst, in0=src, scalar1=qa_abs[:, x:x + 1], scalar2=qa_floor[:, x:x + 1],
                                    op0=ALU.mult, op1=ALU.add)

        def norm_scalar(half, c):
            bank, slot = y_place(half, c)
            for r in range(2):
                nc.scalar.activation(out=y_norm[:, r, :], in_=y_ps[bank][:, slot + r, :], func=ACT.Copy,
                                     scale=rden[bank][:, slot + r:slot + r + 1])

        def gate_gpsimd(half, c):
            g, u = divmod(half, 2)
            nc.gpsimd.tensor_tensor(out=res[g][:, c, u], in0=y_norm[:], in1=gate[g][:, c, u], op=ALU.mult)

        nc.sync.dma_start(out=ka_sb[:], in_=ka)
        load_k(0)
        load_k(1)
        load_k(2)
        load_v(0)
        load_k(3)
        load_q(0)
        load_v(1)
        load_q(1)
        load_og(0)
        load_og(1)
        zero_columns()
        small_loads()
        nc.vector.memset(table_in[:], 0.0)
        nc.scalar.activation(out=table_out[:], in_=table_in[:], func=ACT.Sigmoid)
        relu_k(0, 1)
        relu_k_halves(1)
        relu_k_halves(2)
        cast_v_scalar(0)
        cast_v_scalar(1)
        relu_k(3, 0)
        relu_k(3, 1, 32, R)
        make_tka()
        relu_k_vector(0, 0, 0, 32)
        relu_k_vector(0, 0, 32, R)
        scale_k(0, 0, 0, 32)
        scale_k(0, 0, 32, R)
        scale_k(0, 1)
        make_sign()
        quant_k(0)
        make_abs_floor()
        affine_q_scalar(0, 0)
        affine_q_scalar(0, 1)
        affine_q_scalar(0, 2)
        scale_k(1, 0)
        scale_k(1, 1)
        scale_k(2, 0)
        quant_k(1)
        scale_k(2, 1)
        quant_k(2)
        quant_v(0)
        mm_state(0)
        read_state(0)
        cast_v_scalar(2)
        relu_k_vector(3, 1, 0, 32)
        scale_k(3, 0)
        scale_k(3, 1)
        clamp_q(0, 0)
        affine_q_vector(0, 3)
        quant_k(3)
        clamp_q(0, 3)
        clamp_q(0, 1)
        clamp_q(0, 2)
        interleave_q_scalar(0, 80, P)
        affine_q_scalar(1, 0)
        affine_q_scalar(1, 1)
        affine_q_scalar(1, 2)
        cast_v_vector(3)
        interleave_q_vector(0, 0, 80)
        quant_v_head(3)
        mm_state_head(3, True)
        quant_s(0)
        quant_v_head(2)
        mm_state_head(2, False)
        read_state(1)
        interleave_q_vector(1, 0, 96)
        quant_q(0)
        mm_read(0)
        clamp_q(1, 0)
        affine_q_vector(1, 3)
        clamp_q(1, 1)
        interleave_q_vector(1, 96, P)
        clamp_q(1, 3)
        clamp_q(1, 2)
        interleave_q_scalar(3, 40, P)
        sigmoid(0, 1, slice(0, 2))
        sigmoid(0, 0, 0)
        quant_q(1)
        mm_read(1)
        interleave_q_vector(2, 0, P)
        interleave_q_vector(3, 0, 40)
        quant_s(1)
        quant_q(2)
        mm_read(2)
        recip(1, 4)
        recip(0, 4)
        norm_scalar(0, 0)
        gate_gpsimd(0, 0)
        sigmoid(0, 0, 1)
        sigmoid(1, 0, 0)
        sigmoid(1, 1, 0)
        sigmoid(1, 0, 1)
        sigmoid(1, 1, 1)
        store(0, 0, nc.scalar)
        quant_q(3)
        mm_read(3)
        finish(0, 1)
        store(0, 1, nc.sync)
        finish(1, 1)
        store(1, 1, nc.sync)
        recip(2, 2)
        recip(3, 2)
        finish(1, 0)
        store(1, 0, nc.sync)
        finish(2, 0)
        store(2, 0, nc.sync)
        recip(4, 2)
        recip(5, 2)
        finish(2, 1)
        store(2, 1, nc.sync)
        finish(3, 0)
        store(3, 0, nc.sync)
        finish(3, 1)
        store(3, 1, nc.sync)
